import numpy as np
import ml_dtypes


def mxq(x, axis, fmt="e4m3"):
    dtype, down = {"e4m3": (ml_dtypes.float8_e4m3fn, 7), "e5m2": (ml_dtypes.float8_e5m2, 14)}[fmt]
    v = np.moveaxis(np.asarray(x, np.float32).astype(ml_dtypes.bfloat16).astype(np.float64), axis, -1)
    blocks = v.reshape(v.shape[:-1] + (-1, 32))
    amax = np.abs(blocks).max(-1, keepdims=True)
    byte = np.maximum(np.where(amax > 0, np.frexp(amax)[1] - 1 + 127, 0) - down, 1)
    scale = np.exp2(byte - 127.0)
    codes = (blocks / scale).astype(np.float32).astype(dtype).astype(np.float64)
    return np.moveaxis((codes * scale).reshape(v.shape), -1, axis)


WIDE = False


def mx_kscale(k):
    if not WIDE:
        return np.ones(k)
    levels = np.array([10, -10, 5, -5, 0])
    if k % 512:
        return np.exp2(np.random.permutation(np.resize(levels, k // 32))).repeat(32)
    a = np.empty((k // 512, 16))
    for p in range(k // 512):
        a[p, :8] = np.random.permutation(np.resize(levels, 8))
        for g in range(8):
            far = levels[np.abs(levels - a[p, g]) >= 10]
            a[p, g + 8] = far[np.random.randint(len(far))]
    return np.exp2(a.ravel()).repeat(32)


BF16 = ml_dtypes.bfloat16


def bf(x):
    return np.asarray(x, np.float32).astype(BF16)


def f64(x):
    return np.asarray(x).astype(np.float64)


E2M1 = np.array([0.0, 0.5, 1.0, 1.5, 2.0, 3.0, 4.0, 6.0, -0.0, -0.5, -1.0, -1.5, -2.0, -3.0, -4.0, -6.0])


def pack_weight(w, fmt):
    k, n = w.shape
    w = f64(bf(w)).reshape(k // 32, 32, n)
    amax = np.abs(w).max(1)
    if fmt == "e4m3":
        byte = np.frexp(amax)[1] - 1 + 127 - 7
    else:
        mant, ex = np.frexp(amax / 6.0)
        byte = np.where(mant > 0.5, ex, ex - 1) + 127
    byte = np.clip(np.where(amax > 0, byte, 1), 1, 254)
    scaled = (w * np.exp2(127.0 - byte)[:, None, :]).reshape(k, n).astype(np.float32)
    by_word = np.ascontiguousarray(scaled.reshape(k // 512, 128, 4, n).transpose(0, 1, 3, 2))
    if fmt == "e4m3":
        words = by_word.astype(ml_dtypes.float8_e4m3fn).view(np.uint8)
    else:
        c = by_word.astype(ml_dtypes.float4_e2m1fn).view(np.uint8) & 0xF
        words = c[..., 0::2] | (c[..., 1::2] << 4)
    return np.ascontiguousarray(words), np.ascontiguousarray(byte.astype(np.uint8).reshape(k // 512, 16, n))


def unpack_weight(words, scales, fmt):
    g, p, n, _ = words.shape
    if fmt == "e4m3":
        vals = np.ascontiguousarray(words).view(ml_dtypes.float8_e4m3fn).astype(np.float64)
    else:
        nib = np.empty((g, p, n, 4), np.uint8)
        nib[..., 0::2] = words & 0xF
        nib[..., 1::2] = words >> 4
        vals = E2M1[nib]
    vals = vals * np.repeat(np.exp2(scales.astype(np.float64) - 127.0), 8, axis=1)[..., None]
    return vals.transpose(0, 1, 3, 2).reshape(g * 512, n)
def pack4(w):
    words, scales = pack_weight(w, "e2m1")
    return words.reshape(words.shape[0], 128, -1), scales


def unpack4(words, scales):
    return unpack_weight(words.reshape(words.shape[0], 128, -1, 2), scales, "e2m1")


def planes(Y):
    n, m = Y.shape
    b = f64(bf(Y)).reshape(n // 32, 32, m)
    amax = np.abs(b).max(1)
    byte = np.clip(np.where(amax > 0, np.frexp(amax)[1] - 1 + 127 - 7, 1), 1, 254)
    codes = (b * np.exp2(127.0 - byte)[:, None, :]).reshape(n, m).astype(np.float32).astype(ml_dtypes.float8_e4m3fn).view(np.uint8)
    words = codes.reshape(n // 512, 128, 4, m).transpose(0, 1, 3, 2)
    return np.ascontiguousarray(words), np.ascontiguousarray(byte.astype(np.uint8).reshape(n // 512, 16, m))


T, F, H = 1024, 1024, 1536


def setup_inputs():
    s, t = mx_kscale(F), mx_kscale(H)
    colour = np.exp(0.8 * np.random.randn(F))
    loudness = np.exp(0.3 * np.random.randn(T, 1))
    spec = np.hypot(np.random.randn(T, F), np.random.randn(T, F)) * loudness * colour
    in_gain = np.exp(0.1 * np.random.randn(F)) / colour * s
    W1 = np.random.randn(F, H) / np.sqrt(F) / s[:, None] * t[None, :]
    b1 = 0.4 * np.random.randn(H) * t
    W2 = 1.4 * np.random.randn(H, F) / np.sqrt(H) / t[:, None]
    b2 = 0.5 * np.random.randn(F)
    enc_words, enc_scales = pack4(W1)
    mask_words, mask_scales = pack4(W2)
    return {"spec": bf(spec), "in_gain": bf(in_gain),
            "enc_words": enc_words, "enc_scales": enc_scales, "enc_bias": bf(b1),
            "mask_words": mask_words, "mask_scales": mask_scales, "mask_bias": bf(b2)}


def reference(spec, in_gain, enc_words, enc_scales, enc_bias, mask_words, mask_scales, mask_bias):
    X = f64(spec)
    W1 = unpack4(enc_words, enc_scales)
    W2 = unpack4(mask_words, mask_scales)
    E = X * f64(in_gain)
    hid = np.maximum((mxq(E, 1, "e4m3") @ W1) + f64(enc_bias), 0.0)
    Z = (mxq(hid, 1, "e4m3") @ W2) + f64(mask_bias)
    y = X / (1.0 + np.exp(-Z))
    Y = y.T
    words, scales = planes(Y)
    return y, words, scales

@@ -1,0 +1,548 @@
+from contextlib import ExitStack
+
+import concourse.mybir as mybir
+from concourse.masks import make_identity
+
+T, F, H = 1024, 1024, 1536
+FLOPS = 2 * T * F * H * 2
+
+F32 = mybir.dt.float32
+BF16 = mybir.dt.bfloat16
+I32 = mybir.dt.int32
+U32 = mybir.dt.uint32
+U8 = mybir.dt.uint8
+FP8X4 = mybir.dt.float8_e4m3fn_x4
+FP4X4 = mybir.dt.float4_e2m1fn_x4
+ACT = mybir.ActivationFunctionType
+ALU = mybir.AluOpType
+
+P = 128
+KP = 512
+CH = 512
+NCH = T // CH
+GF = F // KP
+GH = H // KP
+TI = CH // P
+NB = 4
+
+
+def tile_masked_spectra_for_mel_h1_kernel(
+    tc, spec, in_gain, enc_words, enc_scales, enc_bias, mask_words, mask_scales, mask_bias, out_0, out_1, out_2
+):
+    nc = tc.nc
+    with ExitStack() as ctx:
+        keep = ctx.enter_context(tc.tile_pool(name="keep", bufs=1))
+        work = ctx.enter_context(tc.tile_pool(name="work", bufs=2))
+        psum = ctx.enter_context(tc.psum_pool(name="psum", bufs=1))
+        ctx.enter_context(tc.manual_schedule())
+
+        used = {"mm": 0, "tr": 0}
+
+        def bank(role, shape, dtype):
+            k = used[role] % NB
+            used[role] = used[role] + 1
+            return psum.tile(shape, dtype, name="%s%d" % (role, k))
+
+        def kept(name, shape, dtype):
+            return keep.tile(shape, dtype, name=name, align_bytes=64)
+
+        x = {(c, g): kept("x%d%d" % (c, g), [P, TI, KP], BF16) for c in range(NCH) for g in range(GF)}
+        x_sorted = {}
+        gain = kept("gain", [P, GF, 4], BF16)
+        b1 = kept("b1", [P, GH, 4], BF16)
+        b2_rows = kept("b2_rows", [P, P], BF16)
+        b2 = kept("b2", [P, F // P], F32)
+        ident = kept("ident", [P, P], F32)
+        ident_bf = kept("ident_bf", [P, P], BF16)
+        warm = kept("warm", [P, 2], F32)
+        w1_raw = [kept("w1_raw%d" % G, [P, GF, 2 * KP], U8) for G in range(GH)]
+        s1_raw = kept("s1_raw", [P, GF, H], U8)
+        w1 = {(G, g): kept("w1_%d%d" % (G, g), [P, 2 * KP], U8) for G in range(GH) for g in range(GF)}
+        s1 = {(G, g): kept("s1_%d%d" % (G, g), [P, KP], U8) for G in range(GH) for g in range(GF)}
+        w2 = kept("w2", [P, GH, 2 * F], U8)
+        s2 = kept("s2", [P, GH, F], U8)
+        e_bf = {}
+        e_q = {(c, g): kept("e_q%d%d" % (c, g), [P, CH], U32) for c in range(NCH) for g in range(GF)}
+        e_s = {(c, g): kept("e_s%d%d" % (c, g), [P, CH], U8) for c in range(NCH) for g in range(GF)}
+        h_q = {(c, G): kept("h_q%d%d" % (c, G), [P, CH], U32) for c in range(NCH) for G in range(GH)}
+        h_s = {(c, G): kept("h_s%d%d" % (c, G), [P, CH], U8) for c in range(NCH) for G in range(GH)}
+        y_s = kept("y_s", [P, GF, T], U8)
+        xt_bank, pre_bank, h_slots, h_il = {}, {}, {}, {}
+        z_bank, mask_t, mask_bank, y, y_bf, yt_bank, yt = {}, {}, {}, {}, {}, {}, {}
+
+        def load_x(c, g):
+            rows = spec[c * CH : (c + 1) * CH, g * KP : (g + 1) * KP]
+            nc.sync.dma_start(out=x[c, g][:], in_=rows.rearrange("(i p) k -> p i k", p=P))
+
+        def load_x_half(c, g, half):
+            r0 = c * CH + 2 * P * half
+            rows = spec[r0 : r0 + 2 * P, g * KP : (g + 1) * KP]
+            nc.sync.dma_start(out=x[c, g][:, 2 * half : 2 * half + 2, :], in_=rows.rearrange("(i p) k -> p i k", p=P))
+
+        def sort_x(c, g):
+            x_sorted[c, g] = work.tile([P, TI, 2, P], F32, name="x_sorted", align_bytes=64)
+            nc.scalar.copy(
+                out=x_sorted[c, g][:], in_=x[c, g][:].bitcast(F32).rearrange("p i (m u) -> p i u m", u=2)
+            )
+
+        def turn_sorted_x(c, g):
+            for half in range(2):
+                xt_bank[c, g, half] = bank("tr", [P, 2, 2 * P], F32)
+                for ii in range(2):
+                    for u in range(2):
+                        nc.tensor.transpose(
+                            xt_bank[c, g, half][:, u, ii * P : (ii + 1) * P],
+                            x_sorted[c, g][:, 2 * half + ii, u, :],
+                            ident[:],
+                        )
+
+        def sort_w1_words(G, g):
+            nc.vector.tensor_copy(
+                out=w1[G, g][:].rearrange("p (t m b) -> p t m b", t=4, b=2),
+                in_=w1_raw[G][:, g, :].rearrange("p (m t b) -> p t m b", t=4, b=2),
+            )
+
+        def sort_w1_scales(G, g):
+            nc.vector.tensor_copy(
+                out=s1[G, g][:].rearrange("p (t m) -> p t m", t=4),
+                in_=s1_raw[:, g, KP * G : KP * (G + 1)].rearrange("p (m t) -> p t m", t=4),
+            )
+
+        def load_w1(G):
+            src = enc_words[:, :, 2 * KP * G : 2 * KP * (G + 1)].rearrange("g p n -> p g n")
+            nc.sync.dma_start(out=w1_raw[G][:].bitcast(I32), in_=src.bitcast(I32))
+
+        def load_scales(plane, scales):
+            for Q in range(4):
+                src = scales[:, 4 * Q : 4 * Q + 4, :].rearrange("g r n -> r g n")
+                nc.sync.dma_start(out=plane[32 * Q : 32 * Q + 4, :, :].bitcast(I32), in_=src.bitcast(I32))
+
+        def sort_w1(G, g):
+            nc.vector.tensor_copy(
+                out=w1[G, g][:].rearrange("p (t m b) -> p t m b", t=4, b=2),
+                in_=w1_raw[G][:, g, :].rearrange("p (m t b) -> p t m b", t=4, b=2),
+            )
+            nc.vector.tensor_copy(
+                out=s1[G, g][:].rearrange("p (t m) -> p t m", t=4),
+                in_=s1_raw[:, g, KP * G : KP * (G + 1)].rearrange("p (m t) -> p t m", t=4),
+            )
+
+        def turn_x(c, g):
+            words = x[c, g][:].bitcast(F32)
+            for half in range(2):
+                xt_bank[c, g, half] = bank("tr", [P, 2, 2 * P], F32)
+                for ii in range(2):
+                    for u in range(2):
+                        nc.tensor.transpose(
+                            xt_bank[c, g, half][:, u, ii * P : (ii + 1) * P],
+                            words[:, 2 * half + ii, u : 2 * P : 2],
+                            ident[:],
+                        )
+
+        def gain_x(c, g, half):
+            if half == 0:
+                e_bf[c, g] = work.tile([P, CH, 4], BF16, name="e_bf", align_bytes=64)
+            nc.vector.tensor_tensor(
+                out=e_bf[c, g][:, 2 * P * half : 2 * P * (half + 1), :].rearrange("p r (u e) -> p r u e", u=2),
+                in0=xt_bank[c, g, half][:].bitcast(BF16).rearrange("p u (r e) -> p r u e", e=2),
+                in1=gain[:, g, :].rearrange("p (u e) -> p u e", u=2).unsqueeze(1).to_broadcast([P, 2 * P, 2, 2]),
+                op=ALU.mult,
+            )
+
+        def quant_e(c, g):
+            nc.vector.quantize_mx(
+                out=e_q[c, g][:].bitcast(FP8X4), scales=e_s[c, g][:], in_=e_bf[c, g][:].rearrange("p r t -> p (r t)")
+            )
+
+        def enc_pass(c, G, t, g):
+            if g == 0:
+                pre_bank[c, G, t] = bank("mm", [P, CH], F32)
+            nc.tensor.matmul_mx(
+                out=pre_bank[c, G, t][:],
+                lhsT=w1[G, g][:, 2 * P * t : 2 * P * (t + 1)].bitcast(FP4X4),
+                lhsT_scale=s1[G, g][:, P * t : P * (t + 1)],
+                rhs=e_q[c, g][:].bitcast(FP8X4),
+                rhs_scale=e_s[c, g][:],
+                start=(g == 0),
+                stop=(g == GF - 1),
+            )
+
+        def relu_slot(c, G, t):
+            if t == 0:
+                h_slots[c, G] = work.tile([P, 4, CH], BF16, name="h_slots", bufs=3, align_bytes=64)
+            nc.scalar.activation(
+                out=h_slots[c, G][:, t, :], in_=pre_bank[c, G, t][:], func=ACT.Relu, bias=b1[:, G, t : t + 1]
+            )
+
+        def encode(c, G):
+            for t in range(4):
+                for g in range(GF):
+                    enc_pass(c, G, t, g)
+                relu_slot(c, G, t)
+
+        def weave_h(c, G, on_scalar):
+            h_il[c, G] = work.tile([P, CH, 4], BF16, name="h_il", align_bytes=64)
+            dst = h_il[c, G][:].rearrange("p (n i) t -> p n t i", i=4)
+            src = h_slots[c, G][:].rearrange("p t (n i) -> p n t i", i=4)
+            if on_scalar:
+                nc.scalar.copy(out=dst, in_=src)
+            else:
+                nc.vector.tensor_copy(out=dst, in_=src)
+
+        def quant_h(c, G):
+            nc.vector.quantize_mx(
+                out=h_q[c, G][:].bitcast(FP8X4), scales=h_s[c, G][:], in_=h_il[c, G][:].rearrange("p n t -> p (n t)")
+            )
+
+        def logits(c, j):
+            z_bank[c, j] = bank("mm", [P, CH], F32)
+            for G in range(GH):
+                nc.tensor.matmul_mx(
+                    out=z_bank[c, j][:],
+                    lhsT=w2[:, G, 2 * P * j : 2 * P * (j + 1)].bitcast(FP4X4),
+                    lhsT_scale=s2[:, G, P * j : P * (j + 1)],
+                    rhs=h_q[c, G][:].bitcast(FP8X4),
+                    rhs_scale=h_s[c, G][:],
+                    start=(G == 0),
+                    stop=(G == GH - 1),
+                )
+
+        def sigmoid(c, j):
+            mask_t[c, j] = work.tile([P, CH], F32, name="mask_t", bufs=4, align_bytes=64)
+            nc.scalar.activation(out=mask_t[c, j][:], in_=z_bank[c, j][:], func=ACT.Sigmoid, bias=b2[:, j : j + 1])
+
+        def turn_mask(c, j):
+            mask_bank[c, j] = bank("tr", [P, TI, P], F32)
+            for i in range(TI):
+                nc.tensor.transpose(mask_bank[c, j][:, i, :], mask_t[c, j][:, i * P : (i + 1) * P], ident[:])
+
+        def apply_mask(c, j):
+            g, jj = divmod(j, 4)
+            if jj == 0:
+                y[c, g] = work.tile([P, TI, KP], F32, name="y", bufs=3, align_bytes=64)
+            cols = slice(jj * P, (jj + 1) * P)
+            nc.vector.tensor_tensor(
+                out=y[c, g][:, :, cols], in0=mask_bank[c, j][:], in1=x[c, g][:, :, cols], op=ALU.mult
+            )
+
+        def store_y(c, g):
+            rows = out_0[c * CH : (c + 1) * CH, g * KP : (g + 1) * KP]
+            nc.sync.dma_start(out=rows.rearrange("(i p) k -> p i k", p=P), in_=y[c, g][:])
+
+        def round_y(c, j, on_scalar):
+            g, jj = divmod(j, 4)
+            if jj == 0:
+                y_bf[c, g] = work.tile([P, TI, 2, 2 * P], BF16, name="y_bf", align_bytes=64)
+            dst = y_bf[c, g][:, :, :, 64 * jj : 64 * (jj + 1)].rearrange("p i u (m e) -> p i u m e", e=2)
+            src = y[c, g][:, :, jj * P : (jj + 1) * P].rearrange("p i (m u e) -> p i u m e", u=2, e=2)
+            if on_scalar:
+                nc.scalar.copy(out=dst, in_=src)
+            else:
+                nc.vector.tensor_copy(out=dst, in_=src)
+
+        def turn_y(c, g, half):
+            words = y_bf[c, g][:].bitcast(F32)
+            yt_bank[c, g, half] = bank("tr", [P, 2, 2 * P], F32)
+            for ii in range(2):
+                for u in range(2):
+                    nc.tensor.transpose(
+                        yt_bank[c, g, half][:, u, ii * P : (ii + 1) * P], words[:, 2 * half + ii, u, :], ident[:]
+                    )
+
+        def weave_y(c, g, half, on_scalar):
+            if half == 0:
+                yt[c, g] = work.tile([P, CH, 2], F32, name="yt", align_bytes=64)
+            dst = yt[c, g][:, 2 * P * half : 2 * P * (half + 1), :]
+            src = yt_bank[c, g, half][:].rearrange("p u r -> p r u")
+            if on_scalar:
+                nc.scalar.copy(out=dst, in_=src)
+            else:
+                nc.vector.tensor_copy(out=dst, in_=src)
+
+        def planes(c, g):
+            y_q = work.tile([P, CH], U32, name="y_q", align_bytes=64)
+            nc.vector.quantize_mx(
+                out=y_q[:].bitcast(FP8X4),
+                scales=y_s[:, g, c * CH : (c + 1) * CH],
+                in_=yt[c, g][:].rearrange("p r u -> p (r u)").bitcast(BF16),
+            )
+            dst = out_1[g, :, c * CH : (c + 1) * CH, :].rearrange("p m t -> p (m t)")
+            nc.sync.dma_start(out=dst.bitcast(I32), in_=y_q[:].bitcast(I32))
+
+        def store_scales():
+            for Q in range(4):
+                dst = out_2[:, 4 * Q : 4 * Q + 4, :].rearrange("g r n -> r g n")
+                queue = nc.scalar if Q % 2 else nc.sync
+                queue.dma_start(out=dst.bitcast(I32), in_=y_s[32 * Q : 32 * Q + 4, :, :].bitcast(I32))
+
+        b2_wide = kept("b2_wide", [P, KP], BF16)
+        zf_bank, zf, mask_f, yf, yf_bf, yft_bank, yft = {}, {}, {}, {}, {}, {}, {}
+
+        def f_logits(c, g, i):
+            zf_bank[i] = bank("mm", [P, KP], F32)
+            for G in range(GH):
+                nc.tensor.matmul_mx(
+                    out=zf_bank[i][:],
+                    lhsT=h_q[c, G][:, P * i : P * (i + 1)].bitcast(FP8X4),
+                    lhsT_scale=h_s[c, G][:, P * i : P * (i + 1)],
+                    rhs=w2[:, G, 2 * KP * g : 2 * KP * (g + 1)].bitcast(FP4X4),
+                    rhs_scale=s2[:, G, KP * g : KP * (g + 1)],
+                    start=(G == 0),
+                    stop=(G == GH - 1),
+                )
+
+        def f_bias(i):
+            zf[i] = work.tile([P, KP], F32, name="zf", bufs=4, align_bytes=64)
+            nc.vector.tensor_tensor(out=zf[i][:], in0=zf_bank[i][:], in1=b2_wide[:], op=ALU.add)
+
+        def f_sigmoid(i):
+            mask_f[i] = work.tile([P, KP], F32, name="mask_t", bufs=4, align_bytes=64)
+            nc.scalar.activation(out=mask_f[i][:], in_=zf[i][:], func=ACT.Sigmoid)
+
+        def f_apply(c, g, i):
+            yf[i] = work.tile([P, KP], F32, name="yf", bufs=4, align_bytes=64)
+            nc.vector.tensor_tensor(out=yf[i][:], in0=mask_f[i][:], in1=x[c, g][:, i, :], op=ALU.mult)
+            r0 = c * CH + i * P
+            nc.sync.dma_start(out=out_0[r0 : r0 + P, g * KP : (g + 1) * KP], in_=yf[i][:])
+
+        def f_round(i, on_scalar):
+            yf_bf[i] = work.tile([P, 2, 2 * P], BF16, name="yf_bf", bufs=4, align_bytes=64)
+            dst = yf_bf[i][:].rearrange("p u (m e) -> p u m e", e=2)
+            src = yf[i][:].rearrange("p (m u e) -> p u m e", u=2, e=2)
+            if on_scalar:
+                nc.scalar.copy(out=dst, in_=src)
+            else:
+                nc.vector.tensor_copy(out=dst, in_=src)
+
+        def f_apply_bf(c, g, i):
+            yf_bf[i] = work.tile([P, 2, 2 * P], BF16, name="yf_bf", bufs=4, align_bytes=64)
+            nc.vector.tensor_tensor(
+                out=yf_bf[i][:].rearrange("p u (m e) -> p u m e", e=2),
+                in0=mask_f[i][:].rearrange("p (m u e) -> p u m e", u=2, e=2),
+                in1=x[c, g][:, i, :].rearrange("p (m u e) -> p u m e", u=2, e=2),
+                op=ALU.mult,
+            )
+
+        def f_turn(i):
+            words = yf_bf[i][:].bitcast(F32)
+            yft_bank[i] = bank("tr", [P, 2, P], F32)
+            for u in range(2):
+                nc.tensor.transpose(yft_bank[i][:, u, :], words[:, u, :], ident[:])
+
+        def f_weave(i, on_scalar):
+            yft[i] = work.tile([P, P, 2], F32, name="yft", bufs=4, align_bytes=64)
+            src = yft_bank[i][:].rearrange("p u r -> p r u")
+            if on_scalar:
+                nc.scalar.copy(out=yft[i][:], in_=src)
+            else:
+                nc.vector.tensor_copy(out=yft[i][:], in_=src)
+
+        def f_planes(c, g, i):
+            y_qf = work.tile([P, P], U32, name="y_qf", bufs=4, align_bytes=64)
+            r0 = c * CH + i * P
+            nc.vector.quantize_mx(
+                out=y_qf[:].bitcast(FP8X4),
+                scales=y_s[:, g, r0 : r0 + P],
+                in_=yft[i][:].rearrange("p r u -> p (r u)").bitcast(BF16),
+            )
+            dst = out_1[g, :, r0 : r0 + P, :].rearrange("p m t -> p (m t)")
+            nc.sync.dma_start(out=dst.bitcast(I32), in_=y_qf[:].bitcast(I32))
+
+        def store_y_cols(c, g, jj0, jj1):
+            rows = out_0[c * CH : (c + 1) * CH, g * KP + jj0 * P : g * KP + jj1 * P]
+            nc.sync.dma_start(out=rows.rearrange("(i p) k -> p i k", p=P), in_=y[c, g][:, :, jj0 * P : jj1 * P])
+
+        half_bank = {}
+
+        def sigmoid_half(c, j, half):
+            if half == 0:
+                mask_t[c, j] = work.tile([P, CH], F32, name="mask_t", bufs=4, align_bytes=64)
+            cols = slice(2 * P * half, 2 * P * (half + 1))
+            nc.scalar.activation(
+                out=mask_t[c, j][:, cols], in_=z_bank[c, j][:, cols], func=ACT.Sigmoid, bias=b2[:, j : j + 1]
+            )
+
+        def turn_mask_half(c, j, half):
+            half_bank[half] = bank("mm", [P, 2, P], F32)
+            for ii in range(2):
+                i = 2 * half + ii
+                nc.tensor.transpose(half_bank[half][:, ii, :], mask_t[c, j][:, i * P : (i + 1) * P], ident[:])
+
+        def apply_half_bf(c, j, half):
+            g, jj = divmod(j, 4)
+            for ii in range(2):
+                i = 2 * half + ii
+                nc.vector.tensor_tensor(
+                    out=y_bf[c, g][:, i, :, 64 * jj : 64 * (jj + 1)].rearrange("p u (m e) -> p u m e", e=2),
+                    in0=half_bank[half][:, ii, :].rearrange("p (m u e) -> p u m e", u=2, e=2),
+                    in1=x[c, g][:, i, jj * P : (jj + 1) * P].rearrange("p (m u e) -> p u m e", u=2, e=2),
+                    op=ALU.mult,
+                )
+
+        def apply_half(c, j, half):
+            g, jj = divmod(j, 4)
+            cols = slice(jj * P, (jj + 1) * P)
+            rows = slice(2 * half, 2 * half + 2)
+            nc.vector.tensor_tensor(
+                out=y[c, g][:, rows, cols], in0=half_bank[half][:], in1=x[c, g][:, rows, cols], op=ALU.mult
+            )
+
+        def planes_half(c, g, half):
+            y_qh = work.tile([P, 2 * P], U32, name="y_qh", align_bytes=64)
+            r0 = c * CH + 2 * P * half
+            nc.vector.quantize_mx(
+                out=y_qh[:].bitcast(FP8X4),
+                scales=y_s[:, g, r0 : r0 + 2 * P],
+                in_=yt[c, g][:, 2 * P * half : 2 * P * (half + 1), :].rearrange("p r u -> p (r u)").bitcast(BF16),
+            )
+            dst = out_1[g, :, r0 : r0 + 2 * P, :].rearrange("p m t -> p (m t)")
+            nc.sync.dma_start(out=dst.bitcast(I32), in_=y_qh[:].bitcast(I32))
+
+        def bias_columns():
+            b2_bank = bank("mm", [P, P], BF16)
+            nc.tensor.transpose(b2_bank[:], b2_rows[:], ident_bf[:])
+            nc.scalar.copy(out=b2[:], in_=b2_bank[:, 0 : F // P])
+
+        nc.vector.memset(s1_raw[:].bitcast(I32), 0)
+        nc.vector.memset(warm[:, 0:1], 0.0)
+        make_identity(nc, ident[:])
+        nc.gpsimd.memset(b2_rows[:], 0.0)
+        make_identity(nc, ident_bf[:])
+        nc.gpsimd.memset(s2[:].bitcast(I32), 0)
+        nc.scalar.dma_start(out=gain[:], in_=in_gain.rearrange("(g p t) -> p g t", p=P, t=4))
+        nc.scalar.activation(out=warm[:, 1:2], in_=warm[:, 0:1], func=ACT.Sigmoid)
+        load_x_half(0, 0, 0)
+        load_x_half(0, 0, 1)
+        load_scales(s1_raw, enc_scales)
+        load_x(0, 1)
+        load_w1(0)
+        load_w1(1)
+        nc.sync.dma_start(out=b1[:], in_=enc_bias.rearrange("(g p t) -> p g t", p=P, t=4))
+        load_w1(2)
+        load_x(1, 0)
+        load_x(1, 1)
+        nc.sync.dma_start(out=b2_rows[0 : F // P, :], in_=mask_bias.rearrange("(j p) -> j p", p=P))
+        load_scales(s2, mask_scales)
+        nc.sync.dma_start(out=w2[:].bitcast(I32), in_=mask_words.rearrange("g p n -> p g n").bitcast(I32))
+
+        turn_x(0, 0)
+        turn_x(0, 1)
+        gain_x(0, 0, 0)
+        sort_w1_scales(0, 0)
+        gain_x(0, 0, 1)
+        sort_w1_scales(0, 1)
+        quant_e(0, 0)
+        sort_w1_words(0, 0)
+        for t in range(4):
+            enc_pass(0, 0, t, 0)
+        gain_x(0, 1, 0)
+        gain_x(0, 1, 1)
+        sort_w1_words(0, 1)
+        quant_e(0, 1)
+        sort_x(1, 0)
+        for t in range(4):
+            enc_pass(0, 0, t, 1)
+            relu_slot(0, 0, t)
+        sort_w1(1, 0)
+        sort_w1(1, 1)
+        turn_sorted_x(1, 0)
+        encode(0, 1)
+        sort_w1(2, 0)
+        sort_w1(2, 1)
+        gain_x(1, 0, 0)
+        gain_x(1, 0, 1)
+        turn_x(1, 1)
+        encode(0, 2)
+        quant_e(1, 0)
+        gain_x(1, 1, 0)
+        gain_x(1, 1, 1)
+        weave_h(0, 0, False)
+        quant_e(1, 1)
+        encode(1, 0)
+        quant_h(0, 0)
+        weave_h(0, 1, False)
+        weave_h(0, 2, False)
+        quant_h(0, 1)
+        encode(1, 1)
+        quant_h(0, 2)
+        weave_h(1, 0, False)
+        encode(1, 2)
+        bias_columns()
+
+        def unit(n):
+            return divmod(n, 8)
+        def group(n):
+            return divmod(n // 4, 2)
+        def step(s):
+            a = 2 * s
+            old = [n for n in (a - 4, a - 3) if n >= 0]
+            for n in old:
+                apply_mask(*unit(n))
+            if old and a % 4 == 2:
+                store_y(*group(a - 3))
+            for n in old:
+                round_y(*unit(n), False)
+            if a >= 8 and a % 4 == 0:
+                planes(*group(a - 8))
+            for n in (a, a + 1):
+                logits(*unit(n))
+                sigmoid(*unit(n))
+            if a >= 6 and a % 4 == 2:
+                turn_y(*group(a - 6), 0)
+                turn_y(*group(a - 6), 1)
+            for n in (a - 2, a - 1):
+                if n >= 0:
+                    turn_mask(*unit(n))
+            if a >= 6 and a % 4 == 2:
+                weave_y(*group(a - 6), 0, True)
+                weave_y(*group(a - 6), 1, True)
+
+        step(0)
+        quant_h(1, 0)
+        weave_h(1, 1, False)
+        step(1)
+        quant_h(1, 1)
+        weave_h(1, 2, False)
+        step(2)
+        quant_h(1, 2)
+        for s in range(3, 7):
+            step(s)
+        apply_mask(1, 2)
+        apply_mask(1, 3)
+        store_y(1, 0)
+        round_y(1, 2, False)
+        round_y(1, 3, False)
+        logits(1, 6)
+        sigmoid(1, 6)
+        turn_mask(1, 4)
+        turn_mask(1, 5)
+        apply_mask(1, 4)
+        apply_mask(1, 5)
+        store_y_cols(1, 1, 0, 2)
+        round_y(1, 4, False)
+        round_y(1, 5, False)
+        logits(1, 7)
+        sigmoid_half(1, 7, 0)
+        sigmoid_half(1, 7, 1)
+        turn_mask(1, 6)
+        turn_y(1, 0, 0)
+        turn_mask_half(1, 7, 0)
+        turn_y(1, 0, 1)
+        turn_mask_half(1, 7, 1)
+        apply_mask(1, 6)
+        apply_half_bf(1, 7, 0)
+        round_y(1, 6, False)
+        apply_half_bf(1, 7, 1)
+        weave_y(1, 0, 0, True)
+        weave_y(1, 0, 1, True)
+        apply_half(1, 7, 0)
+        apply_half(1, 7, 1)
+        store_y_cols(1, 1, 2, 4)
+        turn_y(1, 1, 0)
+        turn_y(1, 1, 1)
+        planes(1, 0)
+        weave_y(1, 1, 0, True)
+        weave_y(1, 1, 1, False)
+        planes_half(1, 1, 0)
+        planes_half(1, 1, 1)
+        store_scales()

@@ -22,7 +22,6 @@ CH = 512
 NCH = T // CH
 GF = F // KP
 GH = H // KP
-TI = CH // P
 NB = 4
 
 
@@ -46,8 +45,10 @@ def tile_masked_spectra_for_mel_h1_kernel(
         def kept(name, shape, dtype):
             return keep.tile(shape, dtype, name=name, align_bytes=64)
 
-        x = {(c, g): kept("x%d%d" % (c, g), [P, TI, KP], BF16) for c in range(NCH) for g in range(GF)}
-        x_sorted = {}
+        pieces = [(c, g, h) for c in range(NCH) for g in range(GF) for h in range(2)]
+        x = {k: kept("x%d%d%d" % k, [P, 2, KP], BF16) for k in pieces}
+        y = {k: kept("y%d%d%d" % k, [P, 2, KP], F32) for k in pieces}
+        y_bf = {k: kept("y_bf%d%d%d" % k, [P, 2, 2, 2 * P], BF16) for k in pieces}
         gain = kept("gain", [P, GF, 4], BF16)
         b1 = kept("b1", [P, GH, 4], BF16)
         b2_rows = kept("b2_rows", [P, P], BF16)
@@ -61,52 +62,20 @@ def tile_masked_spectra_for_mel_h1_kernel(
         s1 = {(G, g): kept("s1_%d%d" % (G, g), [P, KP], U8) for G in range(GH) for g in range(GF)}
         w2 = kept("w2", [P, GH, 2 * F], U8)
         s2 = kept("s2", [P, GH, F], U8)
-        e_bf = {}
         e_q = {(c, g): kept("e_q%d%d" % (c, g), [P, CH], U32) for c in range(NCH) for g in range(GF)}
         e_s = {(c, g): kept("e_s%d%d" % (c, g), [P, CH], U8) for c in range(NCH) for g in range(GF)}
         h_q = {(c, G): kept("h_q%d%d" % (c, G), [P, CH], U32) for c in range(NCH) for G in range(GH)}
         h_s = {(c, G): kept("h_s%d%d" % (c, G), [P, CH], U8) for c in range(NCH) for G in range(GH)}
         y_s = kept("y_s", [P, GF, T], U8)
-        xt_bank, pre_bank, h_slots, h_il = {}, {}, {}, {}
-        z_bank, mask_t, mask_bank, y, y_bf, yt_bank, yt = {}, {}, {}, {}, {}, {}, {}
+        x_sorted, xt_bank, e_bf, pre_bank, h_slots, h_il = {}, {}, {}, {}, {}, {}
+        z_bank, mask_t, mask_bank, yt_bank, yt = {}, {}, {}, {}, {}
 
-        def load_x(c, g):
-            rows = spec[c * CH : (c + 1) * CH, g * KP : (g + 1) * KP]
-            nc.sync.dma_start(out=x[c, g][:], in_=rows.rearrange("(i p) k -> p i k", p=P))
+        def frames(c, h):
+            return slice(c * CH + 2 * P * h, c * CH + 2 * P * (h + 1))
 
-        def load_x_half(c, g, half):
-            r0 = c * CH + 2 * P * half
-            rows = spec[r0 : r0 + 2 * P, g * KP : (g + 1) * KP]
-            nc.sync.dma_start(out=x[c, g][:, 2 * half : 2 * half + 2, :], in_=rows.rearrange("(i p) k -> p i k", p=P))
-
-        def sort_x(c, g):
-            x_sorted[c, g] = work.tile([P, TI, 2, P], F32, name="x_sorted", align_bytes=64)
-            nc.scalar.copy(
-                out=x_sorted[c, g][:], in_=x[c, g][:].bitcast(F32).rearrange("p i (m u) -> p i u m", u=2)
-            )
-
-        def turn_sorted_x(c, g):
-            for half in range(2):
-                xt_bank[c, g, half] = bank("tr", [P, 2, 2 * P], F32)
-                for ii in range(2):
-                    for u in range(2):
-                        nc.tensor.transpose(
-                            xt_bank[c, g, half][:, u, ii * P : (ii + 1) * P],
-                            x_sorted[c, g][:, 2 * half + ii, u, :],
-                            ident[:],
-                        )
-
-        def sort_w1_words(G, g):
-            nc.vector.tensor_copy(
-                out=w1[G, g][:].rearrange("p (t m b) -> p t m b", t=4, b=2),
-                in_=w1_raw[G][:, g, :].rearrange("p (m t b) -> p t m b", t=4, b=2),
-            )
-
-        def sort_w1_scales(G, g):
-            nc.vector.tensor_copy(
-                out=s1[G, g][:].rearrange("p (t m) -> p t m", t=4),
-                in_=s1_raw[:, g, KP * G : KP * (G + 1)].rearrange("p (m t) -> p t m", t=4),
-            )
+        def load_x(c, g, h):
+            rows = spec[frames(c, h), g * KP : (g + 1) * KP]
+            nc.sync.dma_start(out=x[c, g, h][:], in_=rows.rearrange("(i p) k -> p i k", p=P))
 
         def load_w1(G):
             src = enc_words[:, :, 2 * KP * G : 2 * KP * (G + 1)].rearrange("g p n -> p g n")
@@ -117,34 +86,40 @@ def tile_masked_spectra_for_mel_h1_kernel(
                 src = scales[:, 4 * Q : 4 * Q + 4, :].rearrange("g r n -> r g n")
                 nc.sync.dma_start(out=plane[32 * Q : 32 * Q + 4, :, :].bitcast(I32), in_=src.bitcast(I32))
 
-        def sort_w1(G, g):
+        def sort_words(G, g):
             nc.vector.tensor_copy(
                 out=w1[G, g][:].rearrange("p (t m b) -> p t m b", t=4, b=2),
                 in_=w1_raw[G][:, g, :].rearrange("p (m t b) -> p t m b", t=4, b=2),
             )
+
+        def sort_scales(G, g):
             nc.vector.tensor_copy(
                 out=s1[G, g][:].rearrange("p (t m) -> p t m", t=4),
                 in_=s1_raw[:, g, KP * G : KP * (G + 1)].rearrange("p (m t) -> p t m", t=4),
             )
 
-        def turn_x(c, g):
-            words = x[c, g][:].bitcast(F32)
-            for half in range(2):
-                xt_bank[c, g, half] = bank("tr", [P, 2, 2 * P], F32)
-                for ii in range(2):
-                    for u in range(2):
-                        nc.tensor.transpose(
-                            xt_bank[c, g, half][:, u, ii * P : (ii + 1) * P],
-                            words[:, 2 * half + ii, u : 2 * P : 2],
-                            ident[:],
-                        )
+        def sort_x(c, g, h):
+            x_sorted[c, g, h] = work.tile([P, 2, 2, P], F32, name="x_sorted", bufs=4, align_bytes=64)
+            nc.scalar.copy(
+                out=x_sorted[c, g, h][:], in_=x[c, g, h][:].bitcast(F32).rearrange("p i (m u) -> p i u m", u=2)
+            )
 
-        def gain_x(c, g, half):
-            if half == 0:
+        def turn_x(c, g, h):
+            xt_bank[c, g, h] = bank("tr", [P, 2, 2 * P], F32)
+            for i in range(2):
+                for u in range(2):
+                    if (c, g, h) in x_sorted:
+                        src = x_sorted[c, g, h][:, i, u, :]
+                    else:
+                        src = x[c, g, h][:].bitcast(F32)[:, i, u : 2 * P : 2]
+                    nc.tensor.transpose(xt_bank[c, g, h][:, u, i * P : (i + 1) * P], src, ident[:])
+
+        def gain_x(c, g, h):
+            if h == 0:
                 e_bf[c, g] = work.tile([P, CH, 4], BF16, name="e_bf", align_bytes=64)
             nc.vector.tensor_tensor(
-                out=e_bf[c, g][:, 2 * P * half : 2 * P * (half + 1), :].rearrange("p r (u e) -> p r u e", u=2),
-                in0=xt_bank[c, g, half][:].bitcast(BF16).rearrange("p u (r e) -> p r u e", e=2),
+                out=e_bf[c, g][:, 2 * P * h : 2 * P * (h + 1), :].rearrange("p r (u e) -> p r u e", u=2),
+                in0=xt_bank[c, g, h][:].bitcast(BF16).rearrange("p u (r e) -> p r u e", e=2),
                 in1=gain[:, g, :].rearrange("p (u e) -> p u e", u=2).unsqueeze(1).to_broadcast([P, 2 * P, 2, 2]),
                 op=ALU.mult,
             )
@@ -180,14 +155,21 @@ def tile_masked_spectra_for_mel_h1_kernel(
                     enc_pass(c, G, t, g)
                 relu_slot(c, G, t)
 
-        def weave_h(c, G, on_scalar):
+        def enc_first(c, G):
+            for t in range(4):
+                enc_pass(c, G, t, 0)
+
+        def enc_second(c, G):
+            for t in range(4):
+                enc_pass(c, G, t, 1)
+                relu_slot(c, G, t)
+
+        def weave_h(c, G):
             h_il[c, G] = work.tile([P, CH, 4], BF16, name="h_il", align_bytes=64)
-            dst = h_il[c, G][:].rearrange("p (n i) t -> p n t i", i=4)
-            src = h_slots[c, G][:].rearrange("p t (n i) -> p n t i", i=4)
-            if on_scalar:
-                nc.scalar.copy(out=dst, in_=src)
-            else:
-                nc.vector.tensor_copy(out=dst, in_=src)
+            nc.vector.tensor_copy(
+                out=h_il[c, G][:].rearrange("p (n i) t -> p n t i", i=4),
+                in_=h_slots[c, G][:].rearrange("p t (n i) -> p n t i", i=4),
+            )
 
         def quant_h(c, G):
             nc.vector.quantize_mx(
@@ -206,67 +188,87 @@ def tile_masked_spectra_for_mel_h1_kernel(
                     start=(G == 0),
                     stop=(G == GH - 1),
                 )
+            mask_t[c, j] = work.tile([P, CH], F32, name="mask_t", bufs=8, align_bytes=64)
 
-        def sigmoid(c, j):
-            mask_t[c, j] = work.tile([P, CH], F32, name="mask_t", bufs=4, align_bytes=64)
-            nc.scalar.activation(out=mask_t[c, j][:], in_=z_bank[c, j][:], func=ACT.Sigmoid, bias=b2[:, j : j + 1])
-
-        def turn_mask(c, j):
-            mask_bank[c, j] = bank("tr", [P, TI, P], F32)
-            for i in range(TI):
-                nc.tensor.transpose(mask_bank[c, j][:, i, :], mask_t[c, j][:, i * P : (i + 1) * P], ident[:])
-
-        def apply_mask(c, j):
-            g, jj = divmod(j, 4)
-            if jj == 0:
-                y[c, g] = work.tile([P, TI, KP], F32, name="y", bufs=3, align_bytes=64)
-            cols = slice(jj * P, (jj + 1) * P)
-            nc.vector.tensor_tensor(
-                out=y[c, g][:, :, cols], in0=mask_bank[c, j][:], in1=x[c, g][:, :, cols], op=ALU.mult
+        def sigmoid(c, j, lo=0, hi=CH):
+            nc.scalar.activation(
+                out=mask_t[c, j][:, lo:hi], in_=z_bank[c, j][:, lo:hi], func=ACT.Sigmoid, bias=b2[:, j : j + 1]
             )
 
-        def store_y(c, g):
-            rows = out_0[c * CH : (c + 1) * CH, g * KP : (g + 1) * KP]
-            nc.sync.dma_start(out=rows.rearrange("(i p) k -> p i k", p=P), in_=y[c, g][:])
+        def masks(c, j0, j1):
+            for j in range(j0, j1):
+                logits(c, j)
+                sigmoid(c, j)
 
-        def round_y(c, j, on_scalar):
-            g, jj = divmod(j, 4)
-            if jj == 0:
-                y_bf[c, g] = work.tile([P, TI, 2, 2 * P], BF16, name="y_bf", align_bytes=64)
-            dst = y_bf[c, g][:, :, :, 64 * jj : 64 * (jj + 1)].rearrange("p i u (m e) -> p i u m e", e=2)
-            src = y[c, g][:, :, jj * P : (jj + 1) * P].rearrange("p i (m u e) -> p i u m e", u=2, e=2)
-            if on_scalar:
-                nc.scalar.copy(out=dst, in_=src)
-            else:
-                nc.vector.tensor_copy(out=dst, in_=src)
-
-        def turn_y(c, g, half):
-            words = y_bf[c, g][:].bitcast(F32)
-            yt_bank[c, g, half] = bank("tr", [P, 2, 2 * P], F32)
-            for ii in range(2):
-                for u in range(2):
+        def turn_mask(blk, role="tr"):
+            c, g, h, i0, i1, j0, j1 = blk
+            mask_bank[blk] = bank(role, [P, i1 - i0, (j1 - j0) * P], F32)
+            for i in range(i0, i1):
+                r0 = (2 * h + i) * P
+                for j in range(j0, j1):
                     nc.tensor.transpose(
-                        yt_bank[c, g, half][:, u, ii * P : (ii + 1) * P], words[:, 2 * half + ii, u, :], ident[:]
+                        mask_bank[blk][:, i - i0, (j - j0) * P : (j - j0 + 1) * P],
+                        mask_t[c, 4 * g + j][:, r0 : r0 + P],
+                        ident[:],
                     )
 
-        def weave_y(c, g, half, on_scalar):
-            if half == 0:
-                yt[c, g] = work.tile([P, CH, 2], F32, name="yt", align_bytes=64)
-            dst = yt[c, g][:, 2 * P * half : 2 * P * (half + 1), :]
-            src = yt_bank[c, g, half][:].rearrange("p u r -> p r u")
+        def apply_mask(blk):
+            c, g, h, i0, i1, j0, j1 = blk
+            nc.vector.tensor_tensor(
+                out=y[c, g, h][:, i0:i1, j0 * P : j1 * P],
+                in0=mask_bank[blk][:],
+                in1=x[c, g, h][:, i0:i1, j0 * P : j1 * P],
+                op=ALU.mult,
+            )
+
+        def apply_mask_bf(blk):
+            c, g, h, i0, i1, j0, j1 = blk
+            for i in range(i0, i1):
+                nc.vector.tensor_tensor(
+                    out=y_bf[c, g, h][:, i, :, 64 * j0 : 64 * j1].rearrange("p u (m e) -> p u m e", e=2),
+                    in0=mask_bank[blk][:, i - i0, :].rearrange("p (m u e) -> p u m e", u=2, e=2),
+                    in1=x[c, g, h][:, i, j0 * P : j1 * P].rearrange("p (m u e) -> p u m e", u=2, e=2),
+                    op=ALU.mult,
+                )
+
+        def round_y(blk, on_scalar=False):
+            c, g, h, i0, i1, j0, j1 = blk
+            dst = y_bf[c, g, h][:, i0:i1, :, 64 * j0 : 64 * j1].rearrange("p i u (m e) -> p i u m e", e=2)
+            src = y[c, g, h][:, i0:i1, j0 * P : j1 * P].rearrange("p i (m u e) -> p i u m e", u=2, e=2)
             if on_scalar:
                 nc.scalar.copy(out=dst, in_=src)
             else:
                 nc.vector.tensor_copy(out=dst, in_=src)
 
-        def planes(c, g):
-            y_q = work.tile([P, CH], U32, name="y_q", align_bytes=64)
+        def store_y(c, g, h, j0=0, j1=4):
+            rows = out_0[frames(c, h), g * KP + j0 * P : g * KP + j1 * P]
+            nc.sync.dma_start(out=rows.rearrange("(i p) k -> p i k", p=P), in_=y[c, g, h][:, :, j0 * P : j1 * P])
+
+        def turn_y(c, g, h, role="mm"):
+            words = y_bf[c, g, h][:].bitcast(F32)
+            yt_bank[c, g, h] = bank(role, [P, 2, 2 * P], F32)
+            for i in range(2):
+                for u in range(2):
+                    nc.tensor.transpose(yt_bank[c, g, h][:, u, i * P : (i + 1) * P], words[:, i, u, :], ident[:])
+
+        def weave_y(c, g, h, on_scalar=True):
+            if h == 0:
+                yt[c, g] = work.tile([P, CH, 2], F32, name="yt", bufs=3, align_bytes=64)
+            dst = yt[c, g][:, 2 * P * h : 2 * P * (h + 1), :]
+            src = yt_bank[c, g, h][:].rearrange("p u r -> p r u")
+            if on_scalar:
+                nc.scalar.copy(out=dst, in_=src)
+            else:
+                nc.vector.tensor_copy(out=dst, in_=src)
+
+        def planes(c, g, lo=0, hi=CH):
+            y_q = work.tile([P, hi - lo], U32, name="y_q", bufs=4, align_bytes=64)
             nc.vector.quantize_mx(
                 out=y_q[:].bitcast(FP8X4),
-                scales=y_s[:, g, c * CH : (c + 1) * CH],
-                in_=yt[c, g][:].rearrange("p r u -> p (r u)").bitcast(BF16),
+                scales=y_s[:, g, c * CH + lo : c * CH + hi],
+                in_=yt[c, g][:, lo:hi, :].rearrange("p r u -> p (r u)").bitcast(BF16),
             )
-            dst = out_1[g, :, c * CH : (c + 1) * CH, :].rearrange("p m t -> p (m t)")
+            dst = out_1[g, :, c * CH + lo : c * CH + hi, :].rearrange("p m t -> p (m t)")
             nc.sync.dma_start(out=dst.bitcast(I32), in_=y_q[:].bitcast(I32))
 
         def store_scales():
@@ -275,128 +277,92 @@ def tile_masked_spectra_for_mel_h1_kernel(
                 queue = nc.scalar if Q % 2 else nc.sync
                 queue.dma_start(out=dst.bitcast(I32), in_=y_s[32 * Q : 32 * Q + 4, :, :].bitcast(I32))
 
-        b2_wide = kept("b2_wide", [P, KP], BF16)
-        zf_bank, zf, mask_f, yf, yf_bf, yft_bank, yft = {}, {}, {}, {}, {}, {}, {}
+        b2_wide = kept("b2_wide", [P, F], BF16)
+        zf_bank, zf, mask_f = {}, {}, {}
 
-        def f_logits(c, g, i):
-            zf_bank[i] = bank("mm", [P, KP], F32)
+        def row_logits(u):
+            c, g, h, i = u
+            r0 = (2 * h + i) * P
+            zf_bank[u] = bank("mm", [P, KP], F32)
             for G in range(GH):
                 nc.tensor.matmul_mx(
-                    out=zf_bank[i][:],
-                    lhsT=h_q[c, G][:, P * i : P * (i + 1)].bitcast(FP8X4),
-                    lhsT_scale=h_s[c, G][:, P * i : P * (i + 1)],
+                    out=zf_bank[u][:],
+                    lhsT=h_q[c, G][:, r0 : r0 + P].bitcast(FP8X4),
+                    lhsT_scale=h_s[c, G][:, r0 : r0 + P],
                     rhs=w2[:, G, 2 * KP * g : 2 * KP * (g + 1)].bitcast(FP4X4),
                     rhs_scale=s2[:, G, KP * g : KP * (g + 1)],
                     start=(G == 0),
                     stop=(G == GH - 1),
                 )
 
-        def f_bias(i):
-            zf[i] = work.tile([P, KP], F32, name="zf", bufs=4, align_bytes=64)
-            nc.vector.tensor_tensor(out=zf[i][:], in0=zf_bank[i][:], in1=b2_wide[:], op=ALU.add)
-
-        def f_sigmoid(i):
-            mask_f[i] = work.tile([P, KP], F32, name="mask_t", bufs=4, align_bytes=64)
-            nc.scalar.activation(out=mask_f[i][:], in_=zf[i][:], func=ACT.Sigmoid)
-
-        def f_apply(c, g, i):
-            yf[i] = work.tile([P, KP], F32, name="yf", bufs=4, align_bytes=64)
-            nc.vector.tensor_tensor(out=yf[i][:], in0=mask_f[i][:], in1=x[c, g][:, i, :], op=ALU.mult)
-            r0 = c * CH + i * P
-            nc.sync.dma_start(out=out_0[r0 : r0 + P, g * KP : (g + 1) * KP], in_=yf[i][:])
-
-        def f_round(i, on_scalar):
-            yf_bf[i] = work.tile([P, 2, 2 * P], BF16, name="yf_bf", bufs=4, align_bytes=64)
-            dst = yf_bf[i][:].rearrange("p u (m e) -> p u m e", e=2)
-            src = yf[i][:].rearrange("p (m u e) -> p u m e", u=2, e=2)
-            if on_scalar:
-                nc.scalar.copy(out=dst, in_=src)
-            else:
-                nc.vector.tensor_copy(out=dst, in_=src)
-
-        def f_apply_bf(c, g, i):
-            yf_bf[i] = work.tile([P, 2, 2 * P], BF16, name="yf_bf", bufs=4, align_bytes=64)
+        def row_bias(u, lo=0, hi=KP):
+            if lo == 0:
+                zf[u] = work.tile([P, KP], F32, name="zf", bufs=3, align_bytes=64)
+            g = u[1]
             nc.vector.tensor_tensor(
-                out=yf_bf[i][:].rearrange("p u (m e) -> p u m e", e=2),
-                in0=mask_f[i][:].rearrange("p (m u e) -> p u m e", u=2, e=2),
-                in1=x[c, g][:, i, :].rearrange("p (m u e) -> p u m e", u=2, e=2),
+                out=zf[u][:, lo:hi], in0=zf_bank[u][:, lo:hi], in1=b2_wide[:, g * KP + lo : g * KP + hi], op=ALU.add
+            )
+
+        def row_sigmoid(u, lo=0, hi=KP):
+            if lo == 0:
+                mask_f[u] = work.tile([P, KP], F32, name="mask_t", bufs=8, align_bytes=64)
+            nc.scalar.activation(out=mask_f[u][:, lo:hi], in_=zf[u][:, lo:hi], func=ACT.Sigmoid)
+
+        def row_apply(u):
+            c, g, h, i = u
+            nc.vector.tensor_tensor(out=y[c, g, h][:, i, :], in0=mask_f[u][:], in1=x[c, g, h][:, i, :], op=ALU.mult)
+            r0 = c * CH + (2 * h + i) * P
+            nc.sync.dma_start(out=out_0[r0 : r0 + P, g * KP : (g + 1) * KP], in_=y[c, g, h][:, i, :])
+
+        def row_apply_bf(u, lo=0, hi=KP):
+            c, g, h, i = u
+            nc.vector.tensor_tensor(
+                out=y_bf[c, g, h][:, i, :, lo // 2 : hi // 2].rearrange("p u (m e) -> p u m e", e=2),
+                in0=mask_f[u][:, lo:hi].rearrange("p (m u e) -> p u m e", u=2, e=2),
+                in1=x[c, g, h][:, i, lo:hi].rearrange("p (m u e) -> p u m e", u=2, e=2),
                 op=ALU.mult,
             )
 
-        def f_turn(i):
-            words = yf_bf[i][:].bitcast(F32)
-            yft_bank[i] = bank("tr", [P, 2, P], F32)
-            for u in range(2):
-                nc.tensor.transpose(yft_bank[i][:, u, :], words[:, u, :], ident[:])
+        def row_round(u, on_scalar):
+            c, g, h, i = u
+            round_y((c, g, h, i, i + 1, 0, 4), on_scalar)
 
-        def f_weave(i, on_scalar):
-            yft[i] = work.tile([P, P, 2], F32, name="yft", bufs=4, align_bytes=64)
-            src = yft_bank[i][:].rearrange("p u r -> p r u")
+        def row_turn(u):
+            c, g, h, i = u
+            words = y_bf[c, g, h][:].bitcast(F32)
+            yt_bank[u] = bank("tr", [P, 2, P], F32)
+            for v in range(2):
+                nc.tensor.transpose(yt_bank[u][:, v, :], words[:, i, v, :], ident[:])
+
+        def row_weave(u, on_scalar=True):
+            c, g, h, i = u
+            if (c, g) not in yt:
+                yt[c, g] = work.tile([P, CH, 2], F32, name="yt", bufs=3, align_bytes=64)
+            r0 = (2 * h + i) * P
+            src = yt_bank[u][:].rearrange("p u r -> p r u")
             if on_scalar:
-                nc.scalar.copy(out=yft[i][:], in_=src)
+                nc.scalar.copy(out=yt[c, g][:, r0 : r0 + P, :], in_=src)
             else:
-                nc.vector.tensor_copy(out=yft[i][:], in_=src)
+                nc.vector.tensor_copy(out=yt[c, g][:, r0 : r0 + P, :], in_=src)
 
-        def f_planes(c, g, i):
-            y_qf = work.tile([P, P], U32, name="y_qf", bufs=4, align_bytes=64)
-            r0 = c * CH + i * P
-            nc.vector.quantize_mx(
-                out=y_qf[:].bitcast(FP8X4),
-                scales=y_s[:, g, r0 : r0 + P],
-                in_=yft[i][:].rearrange("p r u -> p (r u)").bitcast(BF16),
-            )
-            dst = out_1[g, :, r0 : r0 + P, :].rearrange("p m t -> p (m t)")
-            nc.sync.dma_start(out=dst.bitcast(I32), in_=y_qf[:].bitcast(I32))
+        def row_planes(u):
+            c, g, h, i = u
+            r0 = (2 * h + i) * P
+            planes(c, g, r0, r0 + P)
 
-        def store_y_cols(c, g, jj0, jj1):
-            rows = out_0[c * CH : (c + 1) * CH, g * KP + jj0 * P : g * KP + jj1 * P]
-            nc.sync.dma_start(out=rows.rearrange("(i p) k -> p i k", p=P), in_=y[c, g][:, :, jj0 * P : jj1 * P])
+        def turn_col(c, g, j, role="tr"):
+            col = bank(role, [P, 4, P], F32)
+            for n in range(4):
+                nc.tensor.transpose(col[:, n, :], mask_t[c, 4 * g + j][:, n * P : (n + 1) * P], ident[:])
+            for h in range(2):
+                mask_bank[c, g, h, 0, 2, j, j + 1] = col[:, 2 * h : 2 * h + 2, :]
 
-        half_bank = {}
-
-        def sigmoid_half(c, j, half):
-            if half == 0:
-                mask_t[c, j] = work.tile([P, CH], F32, name="mask_t", bufs=4, align_bytes=64)
-            cols = slice(2 * P * half, 2 * P * (half + 1))
-            nc.scalar.activation(
-                out=mask_t[c, j][:, cols], in_=z_bank[c, j][:, cols], func=ACT.Sigmoid, bias=b2[:, j : j + 1]
-            )
-
-        def turn_mask_half(c, j, half):
-            half_bank[half] = bank("mm", [P, 2, P], F32)
-            for ii in range(2):
-                i = 2 * half + ii
-                nc.tensor.transpose(half_bank[half][:, ii, :], mask_t[c, j][:, i * P : (i + 1) * P], ident[:])
-
-        def apply_half_bf(c, j, half):
-            g, jj = divmod(j, 4)
-            for ii in range(2):
-                i = 2 * half + ii
-                nc.vector.tensor_tensor(
-                    out=y_bf[c, g][:, i, :, 64 * jj : 64 * (jj + 1)].rearrange("p u (m e) -> p u m e", e=2),
-                    in0=half_bank[half][:, ii, :].rearrange("p (m u e) -> p u m e", u=2, e=2),
-                    in1=x[c, g][:, i, jj * P : (jj + 1) * P].rearrange("p (m u e) -> p u m e", u=2, e=2),
-                    op=ALU.mult,
-                )
-
-        def apply_half(c, j, half):
-            g, jj = divmod(j, 4)
-            cols = slice(jj * P, (jj + 1) * P)
-            rows = slice(2 * half, 2 * half + 2)
-            nc.vector.tensor_tensor(
-                out=y[c, g][:, rows, cols], in0=half_bank[half][:], in1=x[c, g][:, rows, cols], op=ALU.mult
-            )
-
-        def planes_half(c, g, half):
-            y_qh = work.tile([P, 2 * P], U32, name="y_qh", align_bytes=64)
-            r0 = c * CH + 2 * P * half
-            nc.vector.quantize_mx(
-                out=y_qh[:].bitcast(FP8X4),
-                scales=y_s[:, g, r0 : r0 + 2 * P],
-                in_=yt[c, g][:, 2 * P * half : 2 * P * (half + 1), :].rearrange("p r u -> p (r u)").bitcast(BF16),
-            )
-            dst = out_1[g, :, r0 : r0 + 2 * P, :].rearrange("p m t -> p (m t)")
-            nc.sync.dma_start(out=dst.bitcast(I32), in_=y_qh[:].bitcast(I32))
+        def row_turn_role(u, role):
+            c, g, h, i = u
+            words = y_bf[c, g, h][:].bitcast(F32)
+            yt_bank[u] = bank(role, [P, 2, P], F32)
+            for v in range(2):
+                nc.tensor.transpose(yt_bank[u][:, v, :], words[:, i, v, :], ident[:])
 
         def bias_columns():
             b2_bank = bank("mm", [P, P], BF16)
@@ -411,138 +377,158 @@ def tile_masked_spectra_for_mel_h1_kernel(
         nc.gpsimd.memset(s2[:].bitcast(I32), 0)
         nc.scalar.dma_start(out=gain[:], in_=in_gain.rearrange("(g p t) -> p g t", p=P, t=4))
         nc.scalar.activation(out=warm[:, 1:2], in_=warm[:, 0:1], func=ACT.Sigmoid)
-        load_x_half(0, 0, 0)
-        load_x_half(0, 0, 1)
-        load_scales(s1_raw, enc_scales)
-        load_x(0, 1)
+        load_x(0, 0, 0)
+        load_x(0, 0, 1)
+        load_x(0, 1, 0)
         load_w1(0)
+        load_x(0, 1, 1)
+        load_scales(s1_raw, enc_scales)
         load_w1(1)
         nc.sync.dma_start(out=b1[:], in_=enc_bias.rearrange("(g p t) -> p g t", p=P, t=4))
         load_w1(2)
-        load_x(1, 0)
-        load_x(1, 1)
+        for g in range(GF):
+            for h in range(2):
+                load_x(1, g, h)
         nc.sync.dma_start(out=b2_rows[0 : F // P, :], in_=mask_bias.rearrange("(j p) -> j p", p=P))
         load_scales(s2, mask_scales)
         nc.sync.dma_start(out=w2[:].bitcast(I32), in_=mask_words.rearrange("g p n -> p g n").bitcast(I32))
 
-        turn_x(0, 0)
-        turn_x(0, 1)
+        for g in range(GF):
+            for h in range(2):
+                sort_x(0, g, h)
+                turn_x(0, g, h)
         gain_x(0, 0, 0)
-        sort_w1_scales(0, 0)
         gain_x(0, 0, 1)
-        sort_w1_scales(0, 1)
+        sort_words(0, 0)
         quant_e(0, 0)
-        sort_w1_words(0, 0)
-        for t in range(4):
-            enc_pass(0, 0, t, 0)
+        sort_scales(0, 0)
+        enc_first(0, 0)
         gain_x(0, 1, 0)
         gain_x(0, 1, 1)
-        sort_w1_words(0, 1)
+        sort_words(0, 1)
         quant_e(0, 1)
-        sort_x(1, 0)
-        for t in range(4):
-            enc_pass(0, 0, t, 1)
-            relu_slot(0, 0, t)
-        sort_w1(1, 0)
-        sort_w1(1, 1)
-        turn_sorted_x(1, 0)
+        sort_scales(0, 1)
+        sort_x(1, 0, 0)
+        sort_x(1, 0, 1)
+        enc_second(0, 0)
+        for g in range(GF):
+            sort_words(1, g)
+            sort_scales(1, g)
+        turn_x(1, 0, 0)
+        turn_x(1, 0, 1)
         encode(0, 1)
-        sort_w1(2, 0)
-        sort_w1(2, 1)
+        for g in range(GF):
+            sort_words(2, g)
+            sort_scales(2, g)
         gain_x(1, 0, 0)
         gain_x(1, 0, 1)
-        turn_x(1, 1)
+        turn_x(1, 1, 0)
+        turn_x(1, 1, 1)
+        bias_columns()
         encode(0, 2)
-        quant_e(1, 0)
         gain_x(1, 1, 0)
+        quant_e(1, 0)
         gain_x(1, 1, 1)
-        weave_h(0, 0, False)
         quant_e(1, 1)
+        weave_h(0, 0)
         encode(1, 0)
         quant_h(0, 0)
-        weave_h(0, 1, False)
-        weave_h(0, 2, False)
+        weave_h(0, 1)
+        weave_h(0, 2)
         quant_h(0, 1)
         encode(1, 1)
         quant_h(0, 2)
-        weave_h(1, 0, False)
+        weave_h(1, 0)
         encode(1, 2)
-        bias_columns()
 
-        def unit(n):
-            return divmod(n, 8)
-        def group(n):
-            return divmod(n // 4, 2)
-        def step(s):
-            a = 2 * s
-            old = [n for n in (a - 4, a - 3) if n >= 0]
-            for n in old:
-                apply_mask(*unit(n))
-            if old and a % 4 == 2:
-                store_y(*group(a - 3))
-            for n in old:
-                round_y(*unit(n), False)
-            if a >= 8 and a % 4 == 0:
-                planes(*group(a - 8))
-            for n in (a, a + 1):
-                logits(*unit(n))
-                sigmoid(*unit(n))
-            if a >= 6 and a % 4 == 2:
-                turn_y(*group(a - 6), 0)
-                turn_y(*group(a - 6), 1)
-            for n in (a - 2, a - 1):
-                if n >= 0:
-                    turn_mask(*unit(n))
-            if a >= 6 and a % 4 == 2:
-                weave_y(*group(a - 6), 0, True)
-                weave_y(*group(a - 6), 1, True)
+        def whole(c, g):
+            return [(c, g, h, i, i + 1, 0, 4) for h in range(2) for i in range(2)]
+        def cols(c, g, j0, j1):
+            return [(c, g, h, 0, 2, j0, j1) for h in range(2)]
+        def finish(c, g):
+            for h in range(2):
+                apply_mask((c, g, h, 0, 1, 0, 4))
+                apply_mask((c, g, h, 1, 2, 0, 4))
+                store_y(c, g, h)
+            for h in range(2):
+                round_y((c, g, h, 0, 2, 0, 4))
+        def close(c, g, role="mm"):
+            for h in range(2):
+                turn_y(c, g, h, role)
+                weave_y(c, g, h)
 
-        step(0)
+        def col_done(c, g, j):
+            for b in cols(c, g, j, j + 1):
+                apply_mask(b)
+            for b in cols(c, g, j, j + 1):
+                round_y(b)
+        masks(0, 0, 4)
         quant_h(1, 0)
-        weave_h(1, 1, False)
-        step(1)
+        weave_h(1, 1)
+        weave_h(1, 2)
         quant_h(1, 1)
-        weave_h(1, 2, False)
-        step(2)
         quant_h(1, 2)
-        for s in range(3, 7):
-            step(s)
-        apply_mask(1, 2)
-        apply_mask(1, 3)
-        store_y(1, 0)
-        round_y(1, 2, False)
-        round_y(1, 3, False)
-        logits(1, 6)
-        sigmoid(1, 6)
-        turn_mask(1, 4)
-        turn_mask(1, 5)
-        apply_mask(1, 4)
-        apply_mask(1, 5)
-        store_y_cols(1, 1, 0, 2)
-        round_y(1, 4, False)
-        round_y(1, 5, False)
+        masks(0, 4, 6)
+        for b in whole(0, 0):
+            turn_mask(b)
+        finish(0, 0)
+        masks(0, 6, 8)
+        masks(1, 0, 2)
+        for b in whole(0, 1):
+            turn_mask(b)
+        close(0, 0)
+        finish(0, 1)
+        planes(0, 0)
+        masks(1, 2, 4)
+        for b in cols(1, 0, 0, 2):
+            turn_mask(b)
+        turn_col(1, 0, 2)
+        for b in cols(1, 0, 0, 2):
+            apply_mask(b)
+        for b in cols(1, 0, 0, 2):
+            round_y(b)
+        col_done(1, 0, 2)
+        masks(1, 4, 6)
+        turn_col(1, 0, 3)
+        close(0, 1)
+        turn_col(1, 1, 0)
+        for b in cols(1, 0, 3, 4):
+            apply_mask(b)
+            store_y(*b[:3])
+        for b in cols(1, 0, 3, 4):
+            round_y(b)
+        col_done(1, 1, 0)
+        masks(1, 6, 7)
+        turn_col(1, 1, 1)
+        close(1, 0, "tr")
+        turn_col(1, 1, 2)
+        planes(0, 1)
         logits(1, 7)
-        sigmoid_half(1, 7, 0)
-        sigmoid_half(1, 7, 1)
-        turn_mask(1, 6)
-        turn_y(1, 0, 0)
-        turn_mask_half(1, 7, 0)
-        turn_y(1, 0, 1)
-        turn_mask_half(1, 7, 1)
-        apply_mask(1, 6)
-        apply_half_bf(1, 7, 0)
-        round_y(1, 6, False)
-        apply_half_bf(1, 7, 1)
-        weave_y(1, 0, 0, True)
-        weave_y(1, 0, 1, True)
-        apply_half(1, 7, 0)
-        apply_half(1, 7, 1)
-        store_y_cols(1, 1, 2, 4)
-        turn_y(1, 1, 0)
-        turn_y(1, 1, 1)
+        sigmoid(1, 7, 0, 256)
+        sigmoid(1, 7, 256, 512)
+        for b in cols(1, 1, 1, 2):
+            apply_mask(b)
+            store_y(*b[:3], 0, 2)
+        for b in cols(1, 1, 1, 2):
+            round_y(b)
+        for b in cols(1, 1, 2, 3):
+            apply_mask(b)
+            store_y(*b[:3], 2, 3)
+        for b in cols(1, 1, 2, 3):
+            round_y(b)
         planes(1, 0)
-        weave_y(1, 1, 0, True)
-        weave_y(1, 1, 1, False)
-        planes_half(1, 1, 0)
-        planes_half(1, 1, 1)
+        for b in cols(1, 1, 3, 4):
+            turn_mask(b, "mm")
+        last = [(1, 1, h, i) for h in range(2) for i in range(2)]
+        for b in cols(1, 1, 3, 4):
+            apply_mask_bf(b)
+        for u in last:
+            row_turn(u)
+        for b in cols(1, 1, 3, 4):
+            apply_mask(b)
+            store_y(*b[:3], 3, 4)
+        for n, u in enumerate(last):
+            row_weave(u, n != 2)
+        for h in range(2):
+            planes(1, 1, 256 * h, 256 * h + 256)
         store_scales()

@@ -46,9 +46,26 @@ def tile_masked_spectra_for_mel_h1_kernel(
             return keep.tile(shape, dtype, name=name, align_bytes=64)
 
         pieces = [(c, g, h) for c in range(NCH) for g in range(GF) for h in range(2)]
-        x = {k: kept("x%d%d%d" % k, [P, 2, KP], BF16) for k in pieces}
-        y = {k: kept("y%d%d%d" % k, [P, 2, KP], F32) for k in pieces}
-        y_bf = {k: kept("y_bf%d%d%d" % k, [P, 2, 2, 2 * P], BF16) for k in pieces}
+        x, y, y_bf = {}, {}, {}
+        for c in range(NCH):
+            for g in range(GF):
+                if c == 0:
+                    for h in range(2):
+                        x[c, g, h] = kept("x%d%d%d" % (c, g, h), [P, 2, KP], BF16)
+                        y[c, g, h] = kept("y%d%d%d" % (c, g, h), [P, 2, KP], F32)
+                else:
+                    x[c, g, None] = kept("x%d%d" % (c, g), [P, 4, KP], BF16)
+                    y[c, g, None] = kept("y%d%d" % (c, g), [P, 4, KP], F32)
+                    for h in range(2):
+                        x[c, g, h] = x[c, g, None][:, 2 * h : 2 * h + 2, :]
+                        y[c, g, h] = y[c, g, None][:, 2 * h : 2 * h + 2, :]
+                if (c, g) == (1, 0):
+                    y_bf[c, g, None] = kept("y_bf%d%d" % (c, g), [P, 4, 2, 2 * P], BF16)
+                    for h in range(2):
+                        y_bf[c, g, h] = y_bf[c, g, None][:, 2 * h : 2 * h + 2, :, :]
+                else:
+                    for h in range(2):
+                        y_bf[c, g, h] = kept("y_bf%d%d%d" % (c, g, h), [P, 2, 2, 2 * P], BF16)
         gain = kept("gain", [P, GF, 4], BF16)
         b1 = kept("b1", [P, GH, 4], BF16)
         b2_rows = kept("b2_rows", [P, P], BF16)
@@ -71,6 +88,8 @@ def tile_masked_spectra_for_mel_h1_kernel(
         z_bank, mask_t, mask_bank, yt_bank, yt = {}, {}, {}, {}, {}
 
         def frames(c, h):
+            if h is None:
+                return slice(c * CH, (c + 1) * CH)
             return slice(c * CH + 2 * P * h, c * CH + 2 * P * (h + 1))
 
         def load_x(c, g, h):
@@ -81,10 +100,10 @@ def tile_masked_spectra_for_mel_h1_kernel(
             src = enc_words[:, :, 2 * KP * G : 2 * KP * (G + 1)].rearrange("g p n -> p g n")
             nc.sync.dma_start(out=w1_raw[G][:].bitcast(I32), in_=src.bitcast(I32))
 
-        def load_scales(plane, scales):
+        def load_scales(plane, scales, queue=nc.sync):
             for Q in range(4):
                 src = scales[:, 4 * Q : 4 * Q + 4, :].rearrange("g r n -> r g n")
-                nc.sync.dma_start(out=plane[32 * Q : 32 * Q + 4, :, :].bitcast(I32), in_=src.bitcast(I32))
+                queue.dma_start(out=plane[32 * Q : 32 * Q + 4, :, :].bitcast(I32), in_=src.bitcast(I32))
 
         def sort_words(G, g):
             nc.vector.tensor_copy(
@@ -124,9 +143,11 @@ def tile_masked_spectra_for_mel_h1_kernel(
                 op=ALU.mult,
             )
 
-        def quant_e(c, g):
+        def quant_e(c, g, lo=0, hi=CH):
             nc.vector.quantize_mx(
-                out=e_q[c, g][:].bitcast(FP8X4), scales=e_s[c, g][:], in_=e_bf[c, g][:].rearrange("p r t -> p (r t)")
+                out=e_q[c, g][:, lo:hi].bitcast(FP8X4),
+                scales=e_s[c, g][:, lo:hi],
+                in_=e_bf[c, g][:, lo:hi, :].rearrange("p r t -> p (r t)"),
             )
 
         def enc_pass(c, G, t, g):
@@ -271,11 +292,12 @@ def tile_masked_spectra_for_mel_h1_kernel(
             dst = out_1[g, :, c * CH + lo : c * CH + hi, :].rearrange("p m t -> p (m t)")
             nc.sync.dma_start(out=dst.bitcast(I32), in_=y_q[:].bitcast(I32))
 
-        def store_scales():
+        def store_scales(c, spread):
+            fr = frames(c, None)
             for Q in range(4):
-                dst = out_2[:, 4 * Q : 4 * Q + 4, :].rearrange("g r n -> r g n")
-                queue = nc.scalar if Q % 2 else nc.sync
-                queue.dma_start(out=dst.bitcast(I32), in_=y_s[32 * Q : 32 * Q + 4, :, :].bitcast(I32))
+                dst = out_2[:, 4 * Q : 4 * Q + 4, fr].rearrange("g r n -> r g n")
+                queue = nc.scalar if spread and Q % 2 else nc.sync
+                queue.dma_start(out=dst.bitcast(I32), in_=y_s[32 * Q : 32 * Q + 4, :, fr].bitcast(I32))
 
         b2_wide = kept("b2_wide", [P, F], BF16)
         zf_bank, zf, mask_f = {}, {}, {}
@@ -354,8 +376,7 @@ def tile_masked_spectra_for_mel_h1_kernel(
             col = bank(role, [P, 4, P], F32)
             for n in range(4):
                 nc.tensor.transpose(col[:, n, :], mask_t[c, 4 * g + j][:, n * P : (n + 1) * P], ident[:])
-            for h in range(2):
-                mask_bank[c, g, h, 0, 2, j, j + 1] = col[:, 2 * h : 2 * h + 2, :]
+            mask_bank[c, g, None, 0, 4, j, j + 1] = col
 
         def row_turn_role(u, role):
             c, g, h, i = u
@@ -363,6 +384,23 @@ def tile_masked_spectra_for_mel_h1_kernel(
             yt_bank[u] = bank(role, [P, 2, P], F32)
             for v in range(2):
                 nc.tensor.transpose(yt_bank[u][:, v, :], words[:, i, v, :], ident[:])
+
+        def tile_mask(c, j, n):
+            if n == 0:
+                mask_t[c, j] = work.tile([P, CH], F32, name="mask_t", bufs=8, align_bytes=64)
+            z = bank("mm", [P, P], F32)
+            fr = slice(n * P, (n + 1) * P)
+            for G in range(GH):
+                nc.tensor.matmul_mx(
+                    out=z[:],
+                    lhsT=w2[:, G, 2 * P * j : 2 * P * (j + 1)].bitcast(FP4X4),
+                    lhsT_scale=s2[:, G, P * j : P * (j + 1)],
+                    rhs=h_q[c, G][:, fr].bitcast(FP8X4),
+                    rhs_scale=h_s[c, G][:, fr],
+                    start=(G == 0),
+                    stop=(G == GH - 1),
+                )
+            nc.scalar.activation(out=mask_t[c, j][:, fr], in_=z[:], func=ACT.Sigmoid, bias=b2[:, j : j + 1])
 
         def bias_columns():
             b2_bank = bank("mm", [P, P], BF16)
@@ -385,46 +423,47 @@ def tile_masked_spectra_for_mel_h1_kernel(
         load_scales(s1_raw, enc_scales)
         load_w1(1)
         nc.sync.dma_start(out=b1[:], in_=enc_bias.rearrange("(g p t) -> p g t", p=P, t=4))
+        load_x(1, 0, None)
+        load_x(1, 1, None)
         load_w1(2)
-        for g in range(GF):
-            for h in range(2):
-                load_x(1, g, h)
         nc.sync.dma_start(out=b2_rows[0 : F // P, :], in_=mask_bias.rearrange("(j p) -> j p", p=P))
         load_scales(s2, mask_scales)
         nc.sync.dma_start(out=w2[:].bitcast(I32), in_=mask_words.rearrange("g p n -> p g n").bitcast(I32))
+        nc.sync.dma_start(out=b2_wide[:, KP:], in_=mask_bias[KP:].partition_broadcast(P))
 
         for g in range(GF):
             for h in range(2):
                 sort_x(0, g, h)
                 turn_x(0, g, h)
         gain_x(0, 0, 0)
-        gain_x(0, 0, 1)
         sort_words(0, 0)
-        quant_e(0, 0)
+        gain_x(0, 0, 1)
+        quant_e(0, 0, 0, 256)
+        quant_e(0, 0, 256, 512)
         sort_scales(0, 0)
         enc_first(0, 0)
+        sort_words(0, 1)
         gain_x(0, 1, 0)
         gain_x(0, 1, 1)
-        sort_words(0, 1)
-        quant_e(0, 1)
         sort_scales(0, 1)
-        sort_x(1, 0, 0)
-        sort_x(1, 0, 1)
+        quant_e(0, 1)
+        for g in range(GF):
+            for h in range(2):
+                sort_x(1, g, h)
         enc_second(0, 0)
         for g in range(GF):
             sort_words(1, g)
             sort_scales(1, g)
-        turn_x(1, 0, 0)
-        turn_x(1, 0, 1)
+        for g in range(GF):
+            for h in range(2):
+                turn_x(1, g, h)
+        bias_columns()
         encode(0, 1)
         for g in range(GF):
             sort_words(2, g)
             sort_scales(2, g)
         gain_x(1, 0, 0)
         gain_x(1, 0, 1)
-        turn_x(1, 1, 0)
-        turn_x(1, 1, 1)
-        bias_columns()
         encode(0, 2)
         gain_x(1, 1, 0)
         quant_e(1, 0)
@@ -457,78 +496,87 @@ def tile_masked_spectra_for_mel_h1_kernel(
                 turn_y(c, g, h, role)
                 weave_y(c, g, h)
 
-        def col_done(c, g, j):
-            for b in cols(c, g, j, j + 1):
-                apply_mask(b)
-            for b in cols(c, g, j, j + 1):
-                round_y(b)
+        def col(c, g, j):
+            return (c, g, None, 0, 4, j, j + 1)
+        rows = [(0, 1, h, i) for h in range(2) for i in range(2)]
+        def row_mask(u):
+            row_logits(u)
+            row_bias(u)
+            row_sigmoid(u)
         masks(0, 0, 4)
         quant_h(1, 0)
         weave_h(1, 1)
         weave_h(1, 2)
         quant_h(1, 1)
         quant_h(1, 2)
-        masks(0, 4, 6)
+        for u in rows[:2]:
+            row_mask(u)
         for b in whole(0, 0):
             turn_mask(b)
-        finish(0, 0)
-        masks(0, 6, 8)
+        for b in whole(0, 0):
+            apply_mask(b)
+            if b[3] == 1:
+                store_y(*b[:3])
+        round_y((0, 0, 0, 0, 2, 0, 4), True)
+        for u in rows[2:]:
+            row_mask(u)
+        for u in rows[:2]:
+            row_apply(u)
+        round_y((0, 0, 1, 0, 2, 0, 4))
         masks(1, 0, 2)
-        for b in whole(0, 1):
-            turn_mask(b)
-        close(0, 0)
-        finish(0, 1)
-        planes(0, 0)
+        for u in rows[2:]:
+            row_apply(u)
+        round_y((0, 1, 0, 0, 2, 0, 4))
         masks(1, 2, 4)
+        round_y((0, 1, 1, 0, 2, 0, 4), True)
+        close(0, 0)
         for b in cols(1, 0, 0, 2):
             turn_mask(b)
         turn_col(1, 0, 2)
         for b in cols(1, 0, 0, 2):
             apply_mask(b)
-        for b in cols(1, 0, 0, 2):
-            round_y(b)
-        col_done(1, 0, 2)
+        apply_mask(col(1, 0, 2))
+        store_y(1, 0, None, 0, 3)
+        planes(0, 0)
+        round_y((1, 0, None, 0, 4, 0, 3))
         masks(1, 4, 6)
         turn_col(1, 0, 3)
         close(0, 1)
         turn_col(1, 1, 0)
-        for b in cols(1, 0, 3, 4):
-            apply_mask(b)
-            store_y(*b[:3])
-        for b in cols(1, 0, 3, 4):
-            round_y(b)
-        col_done(1, 1, 0)
+        apply_mask(col(1, 0, 3))
+        store_y(1, 0, None, 3, 4)
+        apply_mask(col(1, 1, 0))
+        round_y(col(1, 0, 3))
         masks(1, 6, 7)
         turn_col(1, 1, 1)
         close(1, 0, "tr")
         turn_col(1, 1, 2)
         planes(0, 1)
-        logits(1, 7)
-        sigmoid(1, 7, 0, 256)
-        sigmoid(1, 7, 256, 512)
-        for b in cols(1, 1, 1, 2):
-            apply_mask(b)
-            store_y(*b[:3], 0, 2)
-        for b in cols(1, 1, 1, 2):
+        store_scales(0, False)
+        for n in range(4):
+            tile_mask(1, 7, n)
+        apply_mask(col(1, 1, 1))
+        store_y(1, 1, None, 0, 2)
+        for b in cols(1, 1, 0, 2):
             round_y(b)
-        for b in cols(1, 1, 2, 3):
-            apply_mask(b)
-            store_y(*b[:3], 2, 3)
-        for b in cols(1, 1, 2, 3):
-            round_y(b)
+        apply_mask(col(1, 1, 2))
+        store_y(1, 1, None, 2, 3)
         planes(1, 0)
-        for b in cols(1, 1, 3, 4):
-            turn_mask(b, "mm")
+        for b in cols(1, 1, 2, 3):
+            round_y(b)
         last = [(1, 1, h, i) for h in range(2) for i in range(2)]
-        for b in cols(1, 1, 3, 4):
+        blocks = [(1, 1, h, i, i + 1, 3, 4) for h in range(2) for i in range(2)]
+        for b in blocks:
+            turn_mask(b, "tr")
+        for b in blocks:
             apply_mask_bf(b)
         for u in last:
-            row_turn(u)
-        for b in cols(1, 1, 3, 4):
+            row_turn_role(u, "mm")
+        for b in blocks:
             apply_mask(b)
-            store_y(*b[:3], 3, 4)
+        store_y(1, 1, None, 3, 4)
         for n, u in enumerate(last):
             row_weave(u, n != 2)
-        for h in range(2):
-            planes(1, 1, 256 * h, 256 * h + 256)
-        store_scales()
+        planes(1, 1, 0, 256)
+        planes(1, 1, 256, 512)
+        store_scales(1, True)

@@ -59,7 +59,7 @@ def tile_masked_spectra_for_mel_h1_kernel(
                     for h in range(2):
                         x[c, g, h] = x[c, g, None][:, 2 * h : 2 * h + 2, :]
                         y[c, g, h] = y[c, g, None][:, 2 * h : 2 * h + 2, :]
-                if (c, g) == (1, 0):
+                if False:
                     y_bf[c, g, None] = kept("y_bf%d%d" % (c, g), [P, 4, 2, 2 * P], BF16)
                     for h in range(2):
                         y_bf[c, g, h] = y_bf[c, g, None][:, 2 * h : 2 * h + 2, :, :]
@@ -75,14 +75,20 @@ def tile_masked_spectra_for_mel_h1_kernel(
         warm = kept("warm", [P, 2], F32)
         w1_raw = [kept("w1_raw%d" % G, [P, GF, 2 * KP], U8) for G in range(GH)]
         s1_raw = kept("s1_raw", [P, GF, H], U8)
-        w1 = {(G, g): kept("w1_%d%d" % (G, g), [P, 2 * KP], U8) for G in range(GH) for g in range(GF)}
-        s1 = {(G, g): kept("s1_%d%d" % (G, g), [P, KP], U8) for G in range(GH) for g in range(GF)}
+        w1 = [kept("w1_%d" % G, [P, GF, 2 * KP], U8) for G in range(GH)]
+        s1 = kept("s1", [P, GH, GF, KP], U8)
         w2 = kept("w2", [P, GH, 2 * F], U8)
         s2 = kept("s2", [P, GH, F], U8)
-        e_q = {(c, g): kept("e_q%d%d" % (c, g), [P, CH], U32) for c in range(NCH) for g in range(GF)}
-        e_s = {(c, g): kept("e_s%d%d" % (c, g), [P, CH], U8) for c in range(NCH) for g in range(GF)}
-        h_q = {(c, G): kept("h_q%d%d" % (c, G), [P, CH], U32) for c in range(NCH) for G in range(GH)}
-        h_s = {(c, G): kept("h_s%d%d" % (c, G), [P, CH], U8) for c in range(NCH) for G in range(GH)}
+        e_qc = [kept("e_q%d" % c, [P, GF * CH], U32) for c in range(NCH)]
+        e_sc = [kept("e_s%d" % c, [P, GF * CH], U8) for c in range(NCH)]
+        h_qc = [kept("h_q%d" % c, [P, GH * CH], U32) for c in range(NCH)]
+        h_sc = [kept("h_s%d" % c, [P, GH * CH], U8) for c in range(NCH)]
+        e_q = {(c, g): e_qc[c][:, g * CH : (g + 1) * CH] for c in range(NCH) for g in range(GF)}
+        e_s = {(c, g): e_sc[c][:, g * CH : (g + 1) * CH] for c in range(NCH) for g in range(GF)}
+        h_q = {(c, G): h_qc[c][:, G * CH : (G + 1) * CH] for c in range(NCH) for G in range(GH)}
+        h_s = {(c, G): h_sc[c][:, G * CH : (G + 1) * CH] for c in range(NCH) for G in range(GH)}
+        e_all = [kept("e_bf%d" % c, [P, GF * CH, 4], BF16) for c in range(NCH)]
+        il_all = [kept("h_il%d" % c, [P, GH * CH, 4], BF16) for c in range(NCH)]
         y_s = kept("y_s", [P, GF, T], U8)
         x_sorted, xt_bank, e_bf, pre_bank, h_slots, h_il = {}, {}, {}, {}, {}, {}
         z_bank, mask_t, mask_bank, yt_bank, yt = {}, {}, {}, {}, {}
@@ -105,16 +111,16 @@ def tile_masked_spectra_for_mel_h1_kernel(
                 src = scales[:, 4 * Q : 4 * Q + 4, :].rearrange("g r n -> r g n")
                 queue.dma_start(out=plane[32 * Q : 32 * Q + 4, :, :].bitcast(I32), in_=src.bitcast(I32))
 
-        def sort_words(G, g):
+        def sort_words(G, g0=0, g1=GF):
             nc.vector.tensor_copy(
-                out=w1[G, g][:].rearrange("p (t m b) -> p t m b", t=4, b=2),
-                in_=w1_raw[G][:, g, :].rearrange("p (m t b) -> p t m b", t=4, b=2),
+                out=w1[G][:, g0:g1, :].rearrange("p g (t m b) -> p g t m b", t=4, b=2),
+                in_=w1_raw[G][:, g0:g1, :].rearrange("p g (m t b) -> p g t m b", t=4, b=2),
             )
 
-        def sort_scales(G, g):
+        def sort_scales(G0, G1):
             nc.vector.tensor_copy(
-                out=s1[G, g][:].rearrange("p (t m) -> p t m", t=4),
-                in_=s1_raw[:, g, KP * G : KP * (G + 1)].rearrange("p (m t) -> p t m", t=4),
+                out=s1[:, G0:G1, :, :].rearrange("p G g (t m) -> p G g t m", t=4),
+                in_=s1_raw[:, :, KP * G0 : KP * G1].rearrange("p g (G m t) -> p G g t m", t=4, m=P),
             )
 
         def sort_x(c, g, h):
@@ -134,8 +140,7 @@ def tile_masked_spectra_for_mel_h1_kernel(
                     nc.tensor.transpose(xt_bank[c, g, h][:, u, i * P : (i + 1) * P], src, ident[:])
 
         def gain_x(c, g, h):
-            if h == 0:
-                e_bf[c, g] = work.tile([P, CH, 4], BF16, name="e_bf", align_bytes=64)
+            e_bf[c, g] = e_all[c][:, g * CH : (g + 1) * CH, :]
             nc.vector.tensor_tensor(
                 out=e_bf[c, g][:, 2 * P * h : 2 * P * (h + 1), :].rearrange("p r (u e) -> p r u e", u=2),
                 in0=xt_bank[c, g, h][:].bitcast(BF16).rearrange("p u (r e) -> p r u e", e=2),
@@ -143,11 +148,11 @@ def tile_masked_spectra_for_mel_h1_kernel(
                 op=ALU.mult,
             )
 
-        def quant_e(c, g, lo=0, hi=CH):
+        def quant_e(c, lo, hi):
             nc.vector.quantize_mx(
-                out=e_q[c, g][:, lo:hi].bitcast(FP8X4),
-                scales=e_s[c, g][:, lo:hi],
-                in_=e_bf[c, g][:, lo:hi, :].rearrange("p r t -> p (r t)"),
+                out=e_qc[c][:, lo:hi].bitcast(FP8X4),
+                scales=e_sc[c][:, lo:hi],
+                in_=e_all[c][:, lo:hi, :].rearrange("p r t -> p (r t)"),
             )
 
         def enc_pass(c, G, t, g):
@@ -155,8 +160,8 @@ def tile_masked_spectra_for_mel_h1_kernel(
                 pre_bank[c, G, t] = bank("mm", [P, CH], F32)
             nc.tensor.matmul_mx(
                 out=pre_bank[c, G, t][:],
-                lhsT=w1[G, g][:, 2 * P * t : 2 * P * (t + 1)].bitcast(FP4X4),
-                lhsT_scale=s1[G, g][:, P * t : P * (t + 1)],
+                lhsT=w1[G][:, g, 2 * P * t : 2 * P * (t + 1)].bitcast(FP4X4),
+                lhsT_scale=s1[:, G, g, P * t : P * (t + 1)],
                 rhs=e_q[c, g][:].bitcast(FP8X4),
                 rhs_scale=e_s[c, g][:],
                 start=(g == 0),
@@ -185,16 +190,19 @@ def tile_masked_spectra_for_mel_h1_kernel(
                 enc_pass(c, G, t, 1)
                 relu_slot(c, G, t)
 
-        def weave_h(c, G):
-            h_il[c, G] = work.tile([P, CH, 4], BF16, name="h_il", align_bytes=64)
-            nc.vector.tensor_copy(
-                out=h_il[c, G][:].rearrange("p (n i) t -> p n t i", i=4),
-                in_=h_slots[c, G][:].rearrange("p t (n i) -> p n t i", i=4),
-            )
+        def weave_h(c, G, on_scalar=False):
+            dst = il_all[c][:, G * CH : (G + 1) * CH, :].rearrange("p (n i) t -> p n t i", i=4)
+            src = h_slots[c, G][:].rearrange("p t (n i) -> p n t i", i=4)
+            if on_scalar:
+                nc.scalar.copy(out=dst, in_=src)
+            else:
+                nc.vector.tensor_copy(out=dst, in_=src)
 
-        def quant_h(c, G):
+        def quant_h(c, G0, G1):
             nc.vector.quantize_mx(
-                out=h_q[c, G][:].bitcast(FP8X4), scales=h_s[c, G][:], in_=h_il[c, G][:].rearrange("p n t -> p (n t)")
+                out=h_qc[c][:, G0 * CH : G1 * CH].bitcast(FP8X4),
+                scales=h_sc[c][:, G0 * CH : G1 * CH],
+                in_=il_all[c][:, G0 * CH : G1 * CH, :].rearrange("p n t -> p (n t)"),
             )
 
         def logits(c, j):
@@ -415,12 +423,12 @@ def tile_masked_spectra_for_mel_h1_kernel(
         nc.gpsimd.memset(s2[:].bitcast(I32), 0)
         nc.scalar.dma_start(out=gain[:], in_=in_gain.rearrange("(g p t) -> p g t", p=P, t=4))
         nc.scalar.activation(out=warm[:, 1:2], in_=warm[:, 0:1], func=ACT.Sigmoid)
+        load_w1(0)
         load_x(0, 0, 0)
         load_x(0, 0, 1)
-        load_x(0, 1, 0)
-        load_w1(0)
-        load_x(0, 1, 1)
         load_scales(s1_raw, enc_scales)
+        load_x(0, 1, 0)
+        load_x(0, 1, 1)
         load_w1(1)
         nc.sync.dma_start(out=b1[:], in_=enc_bias.rearrange("(g p t) -> p g t", p=P, t=4))
         load_x(1, 0, None)
@@ -435,49 +443,43 @@ def tile_masked_spectra_for_mel_h1_kernel(
             for h in range(2):
                 sort_x(0, g, h)
                 turn_x(0, g, h)
+        sort_words(0)
         gain_x(0, 0, 0)
-        sort_words(0, 0)
         gain_x(0, 0, 1)
-        quant_e(0, 0, 0, 256)
-        quant_e(0, 0, 256, 512)
-        sort_scales(0, 0)
+        sort_scales(0, 1)
+        quant_e(0, 0, 512)
         enc_first(0, 0)
-        sort_words(0, 1)
         gain_x(0, 1, 0)
         gain_x(0, 1, 1)
-        sort_scales(0, 1)
-        quant_e(0, 1)
+        sort_scales(1, 2)
+        quant_e(0, 512, 1024)
         for g in range(GF):
             for h in range(2):
                 sort_x(1, g, h)
         enc_second(0, 0)
-        for g in range(GF):
-            sort_words(1, g)
-            sort_scales(1, g)
+        sort_words(1)
+        sort_scales(2, 3)
         for g in range(GF):
             for h in range(2):
                 turn_x(1, g, h)
         bias_columns()
         encode(0, 1)
-        for g in range(GF):
-            sort_words(2, g)
-            sort_scales(2, g)
+        sort_words(2)
         gain_x(1, 0, 0)
         gain_x(1, 0, 1)
         encode(0, 2)
         gain_x(1, 1, 0)
-        quant_e(1, 0)
         gain_x(1, 1, 1)
-        quant_e(1, 1)
+        quant_e(1, 0, 512)
+        quant_e(1, 512, 1024)
         weave_h(0, 0)
         encode(1, 0)
-        quant_h(0, 0)
         weave_h(0, 1)
+        quant_h(0, 0, 1)
         weave_h(0, 2)
-        quant_h(0, 1)
         encode(1, 1)
-        quant_h(0, 2)
         weave_h(1, 0)
+        quant_h(0, 1, 3)
         encode(1, 2)
 
         def whole(c, g):
@@ -498,72 +500,72 @@ def tile_masked_spectra_for_mel_h1_kernel(
 
         def col(c, g, j):
             return (c, g, None, 0, 4, j, j + 1)
+        def half(c, g, h, j0=0, j1=4):
+            return (c, g, h, 0, 2, j0, j1)
         rows = [(0, 1, h, i) for h in range(2) for i in range(2)]
         def row_mask(u):
             row_logits(u)
             row_bias(u)
             row_sigmoid(u)
         masks(0, 0, 4)
-        quant_h(1, 0)
         weave_h(1, 1)
+        quant_h(1, 0, 1)
         weave_h(1, 2)
-        quant_h(1, 1)
-        quant_h(1, 2)
+        quant_h(1, 1, 3)
         for u in rows[:2]:
             row_mask(u)
-        for b in whole(0, 0):
+        first = whole(0, 0)
+        for b in first:
             turn_mask(b)
-        for b in whole(0, 0):
-            apply_mask(b)
-            if b[3] == 1:
-                store_y(*b[:3])
-        round_y((0, 0, 0, 0, 2, 0, 4), True)
-        for u in rows[2:]:
-            row_mask(u)
-        for u in rows[:2]:
+        apply_mask(first[0])
+        apply_mask(first[1])
+        store_y(0, 0, 0)
+        round_y(half(0, 0, 0), True)
+        apply_mask(first[2])
+        row_mask(rows[2])
+        apply_mask(first[3])
+        store_y(0, 0, 1)
+        row_mask(rows[3])
+        round_y(half(0, 0, 1))
+        masks(1, 0, 4)
+        for u in rows:
             row_apply(u)
-        round_y((0, 0, 1, 0, 2, 0, 4))
-        masks(1, 0, 2)
-        for u in rows[2:]:
-            row_apply(u)
-        round_y((0, 1, 0, 0, 2, 0, 4))
-        masks(1, 2, 4)
-        round_y((0, 1, 1, 0, 2, 0, 4), True)
         close(0, 0)
         for b in cols(1, 0, 0, 2):
             turn_mask(b)
         turn_col(1, 0, 2)
+        round_y(half(0, 1, 1), True)
+        round_y(half(0, 1, 0))
         for b in cols(1, 0, 0, 2):
             apply_mask(b)
+        planes(0, 0)
         apply_mask(col(1, 0, 2))
         store_y(1, 0, None, 0, 3)
-        planes(0, 0)
-        round_y((1, 0, None, 0, 4, 0, 3))
         masks(1, 4, 6)
         turn_col(1, 0, 3)
         close(0, 1)
         turn_col(1, 1, 0)
         apply_mask(col(1, 0, 3))
         store_y(1, 0, None, 3, 4)
+        round_y(half(1, 0, 0))
+        round_y(half(1, 0, 1))
         apply_mask(col(1, 1, 0))
-        round_y(col(1, 0, 3))
         masks(1, 6, 7)
         turn_col(1, 1, 1)
         close(1, 0, "tr")
         turn_col(1, 1, 2)
         planes(0, 1)
         store_scales(0, False)
-        for n in range(4):
-            tile_mask(1, 7, n)
         apply_mask(col(1, 1, 1))
         store_y(1, 1, None, 0, 2)
-        for b in cols(1, 1, 0, 2):
-            round_y(b)
+
+        for n in range(4):
+            tile_mask(1, 7, n)
         apply_mask(col(1, 1, 2))
         store_y(1, 1, None, 2, 3)
         planes(1, 0)
-        for b in cols(1, 1, 2, 3):
-            round_y(b)
+        round_y(half(1, 1, 0, 0, 3))
+        round_y(half(1, 1, 1, 0, 3), True)
         last = [(1, 1, h, i) for h in range(2) for i in range(2)]
         blocks = [(1, 1, h, i, i + 1, 3, 4) for h in range(2) for i in range(2)]
         for b in blocks:

@@ -17,12 +17,14 @@ ACT = mybir.ActivationFunctionType
 ALU = mybir.AluOpType
 
 P = 128
-KP = 512
+SLOTS = 4
+KP = P * SLOTS
 CH = 512
-NCH = T // CH
-GF = F // KP
-GH = H // KP
-NB = 4
+HALF = CH // 2
+TILES = CH // P
+NCH, GF, GH = T // CH, F // KP, H // KP
+RING = 4
+Y_PIECES = ([(0, 2), (2, 4)], [(0, 2), (2, 3), (3, 4)])
 
 
 def tile_masked_spectra_for_mel_h1_kernel(
@@ -35,68 +37,66 @@ def tile_masked_spectra_for_mel_h1_kernel(
         psum = ctx.enter_context(tc.psum_pool(name="psum", bufs=1))
         ctx.enter_context(tc.manual_schedule())
 
-        used = {"mm": 0, "tr": 0}
+        taken = {"mm": 0, "tr": 0}
 
-        def bank(role, shape, dtype):
-            k = used[role] % NB
-            used[role] = used[role] + 1
-            return psum.tile(shape, dtype, name="%s%d" % (role, k))
+        def bank(ring, shape, dtype=F32):
+            k = taken[ring] % RING
+            taken[ring] = taken[ring] + 1
+            return psum.tile(shape, dtype, name="%s%d" % (ring, k))
 
         def kept(name, shape, dtype):
             return keep.tile(shape, dtype, name=name, align_bytes=64)
 
-        pieces = [(c, g, h) for c in range(NCH) for g in range(GF) for h in range(2)]
-        x, y, y_bf = {}, {}, {}
-        for c in range(NCH):
-            for g in range(GF):
-                if c == 0:
-                    for h in range(2):
-                        x[c, g, h] = kept("x%d%d%d" % (c, g, h), [P, 2, KP], BF16)
-                        y[c, g, h] = kept("y%d%d%d" % (c, g, h), [P, 2, KP], F32)
-                else:
-                    x[c, g, None] = kept("x%d%d" % (c, g), [P, 4, KP], BF16)
-                    y[c, g, None] = kept("y%d%d" % (c, g), [P, 4, KP], F32)
-                    for h in range(2):
-                        x[c, g, h] = x[c, g, None][:, 2 * h : 2 * h + 2, :]
-                        y[c, g, h] = y[c, g, None][:, 2 * h : 2 * h + 2, :]
-                if False:
-                    y_bf[c, g, None] = kept("y_bf%d%d" % (c, g), [P, 4, 2, 2 * P], BF16)
-                    for h in range(2):
-                        y_bf[c, g, h] = y_bf[c, g, None][:, 2 * h : 2 * h + 2, :, :]
-                else:
-                    for h in range(2):
-                        y_bf[c, g, h] = kept("y_bf%d%d%d" % (c, g, h), [P, 2, 2, 2 * P], BF16)
-        gain = kept("gain", [P, GF, 4], BF16)
-        b1 = kept("b1", [P, GH, 4], BF16)
+        def copy_on(engine, out, in_):
+            if engine == "scalar":
+                nc.scalar.copy(out=out, in_=in_)
+            else:
+                nc.vector.tensor_copy(out=out, in_=in_)
+
+        x, y, y_piece, y_pairs = {}, {}, {}, {}
+        for g in range(GF):
+            for h in range(2):
+                x[0, g, h] = kept("x0%d%d" % (g, h), [P, 2, KP], BF16)
+                y[0, g, h] = kept("y0%d%d" % (g, h), [P, 2, KP], F32)
+                y_pairs[0, g, h] = kept("y_pairs0%d%d" % (g, h), [P, 2, 2, HALF], BF16)
+            x[1, g, None] = kept("x1%d" % g, [P, TILES, KP], BF16)
+            for h in range(2):
+                x[1, g, h] = x[1, g, None][:, 2 * h : 2 * h + 2, :]
+            for ja, jb in Y_PIECES[g]:
+                y_piece[g, ja] = kept("y1%d%d" % (g, ja), [P, TILES, (jb - ja) * P], F32)
+        y_pairs[1, 0, None] = kept("y_pairs10", [P, TILES, 2, HALF], BF16)
+        for h in range(2):
+            y_pairs[1, 0, h] = y_pairs[1, 0, None][:, 2 * h : 2 * h + 2, :, :]
+            y_pairs[1, 1, h] = kept("y_pairs11%d" % h, [P, 2, 2, HALF], BF16)
+
+        gain = kept("gain", [P, GF, SLOTS], BF16)
+        b1 = kept("b1", [P, GH, SLOTS], BF16)
         b2_rows = kept("b2_rows", [P, P], BF16)
-        b2 = kept("b2", [P, F // P], F32)
+        b2_cols = kept("b2_cols", [P, F // P], F32)
+        b2_wide = kept("b2_wide", [P, KP], BF16)
         ident = kept("ident", [P, P], F32)
         ident_bf = kept("ident_bf", [P, P], BF16)
         warm = kept("warm", [P, 2], F32)
         w1_raw = [kept("w1_raw%d" % G, [P, GF, 2 * KP], U8) for G in range(GH)]
         s1_raw = kept("s1_raw", [P, GF, H], U8)
         w1 = [kept("w1_%d" % G, [P, GF, 2 * KP], U8) for G in range(GH)]
-        s1 = kept("s1", [P, GH, GF, KP], U8)
+        s1 = [kept("s1_%d" % G, [P, GF, KP], U8) for G in range(GH)]
         w2 = kept("w2", [P, GH, 2 * F], U8)
         s2 = kept("s2", [P, GH, F], U8)
-        e_qc = [kept("e_q%d" % c, [P, GF * CH], U32) for c in range(NCH)]
-        e_sc = [kept("e_s%d" % c, [P, GF * CH], U8) for c in range(NCH)]
-        h_qc = [kept("h_q%d" % c, [P, GH * CH], U32) for c in range(NCH)]
-        h_sc = [kept("h_s%d" % c, [P, GH * CH], U8) for c in range(NCH)]
-        e_q = {(c, g): e_qc[c][:, g * CH : (g + 1) * CH] for c in range(NCH) for g in range(GF)}
-        e_s = {(c, g): e_sc[c][:, g * CH : (g + 1) * CH] for c in range(NCH) for g in range(GF)}
-        h_q = {(c, G): h_qc[c][:, G * CH : (G + 1) * CH] for c in range(NCH) for G in range(GH)}
-        h_s = {(c, G): h_sc[c][:, G * CH : (G + 1) * CH] for c in range(NCH) for G in range(GH)}
-        e_all = [kept("e_bf%d" % c, [P, GF * CH, 4], BF16) for c in range(NCH)]
-        il_all = [kept("h_il%d" % c, [P, GH * CH, 4], BF16) for c in range(NCH)]
-        y_s = kept("y_s", [P, GF, T], U8)
-        x_sorted, xt_bank, e_bf, pre_bank, h_slots, h_il = {}, {}, {}, {}, {}, {}
-        z_bank, mask_t, mask_bank, yt_bank, yt = {}, {}, {}, {}, {}
+        e_bf = [kept("e_bf%d" % c, [P, GF * CH, SLOTS], BF16) for c in range(NCH)]
+        e_q = [kept("e_q%d" % c, [P, GF * CH], U32) for c in range(NCH)]
+        e_s = [kept("e_s%d" % c, [P, GF * CH], U8) for c in range(NCH)]
+        h_bf = [kept("h_il%d" % c, [P, GH * CH, SLOTS], BF16) for c in range(NCH)]
+        h_q = [kept("h_q%d" % c, [P, GH * CH], U32) for c in range(NCH)]
+        h_s = [kept("h_s%d" % c, [P, GH * CH], U8) for c in range(NCH)]
+        y_s = [kept("y_s%d" % c, [P, GF, CH], U8) for c in range(NCH)]
+        x_pairs, xt_bank, pre_bank, h_slots = {}, {}, {}, {}
+        mask, mask_bank, yt_bank, yt = {}, {}, {}, {}
 
         def frames(c, h):
             if h is None:
                 return slice(c * CH, (c + 1) * CH)
-            return slice(c * CH + 2 * P * h, c * CH + 2 * P * (h + 1))
+            return slice(c * CH + HALF * h, c * CH + HALF * (h + 1))
 
         def load_x(c, g, h):
             rows = spec[frames(c, h), g * KP : (g + 1) * KP]
@@ -106,314 +106,240 @@ def tile_masked_spectra_for_mel_h1_kernel(
             src = enc_words[:, :, 2 * KP * G : 2 * KP * (G + 1)].rearrange("g p n -> p g n")
             nc.sync.dma_start(out=w1_raw[G][:].bitcast(I32), in_=src.bitcast(I32))
 
-        def load_scales(plane, scales, queue=nc.sync):
+        def load_scales(tile, scales):
             for Q in range(4):
                 src = scales[:, 4 * Q : 4 * Q + 4, :].rearrange("g r n -> r g n")
-                queue.dma_start(out=plane[32 * Q : 32 * Q + 4, :, :].bitcast(I32), in_=src.bitcast(I32))
+                nc.sync.dma_start(out=tile[32 * Q : 32 * Q + 4, :, :].bitcast(I32), in_=src.bitcast(I32))
 
-        def sort_words(G, g0=0, g1=GF):
+        def sort_w1_codes(G):
             nc.vector.tensor_copy(
-                out=w1[G][:, g0:g1, :].rearrange("p g (t m b) -> p g t m b", t=4, b=2),
-                in_=w1_raw[G][:, g0:g1, :].rearrange("p g (m t b) -> p g t m b", t=4, b=2),
+                out=w1[G][:].rearrange("p g (t m b) -> p g t m b", t=SLOTS, b=2),
+                in_=w1_raw[G][:].rearrange("p g (m t b) -> p g t m b", t=SLOTS, b=2),
             )
 
-        def sort_scales(G0, G1):
+        def sort_w1_scales(G):
             nc.vector.tensor_copy(
-                out=s1[:, G0:G1, :, :].rearrange("p G g (t m) -> p G g t m", t=4),
-                in_=s1_raw[:, :, KP * G0 : KP * G1].rearrange("p g (G m t) -> p G g t m", t=4, m=P),
+                out=s1[G][:].rearrange("p g (t m) -> p g t m", t=SLOTS),
+                in_=s1_raw[:, :, KP * G : KP * (G + 1)].rearrange("p g (m t) -> p g t m", t=SLOTS),
             )
 
         def sort_x(c, g, h):
-            x_sorted[c, g, h] = work.tile([P, 2, 2, P], F32, name="x_sorted", bufs=4, align_bytes=64)
+            x_pairs[c, g, h] = work.tile([P, 2, 2, P], F32, name="x_sorted", bufs=4, align_bytes=64)
             nc.scalar.copy(
-                out=x_sorted[c, g, h][:], in_=x[c, g, h][:].bitcast(F32).rearrange("p i (m u) -> p i u m", u=2)
+                out=x_pairs[c, g, h][:], in_=x[c, g, h][:].bitcast(F32).rearrange("p i (m u) -> p i u m", u=2)
             )
 
         def turn_x(c, g, h):
-            xt_bank[c, g, h] = bank("tr", [P, 2, 2 * P], F32)
+            xt_bank[c, g, h] = bank("tr", [P, 2, HALF])
             for i in range(2):
                 for u in range(2):
-                    if (c, g, h) in x_sorted:
-                        src = x_sorted[c, g, h][:, i, u, :]
-                    else:
-                        src = x[c, g, h][:].bitcast(F32)[:, i, u : 2 * P : 2]
-                    nc.tensor.transpose(xt_bank[c, g, h][:, u, i * P : (i + 1) * P], src, ident[:])
+                    nc.tensor.transpose(
+                        xt_bank[c, g, h][:, u, i * P : (i + 1) * P], x_pairs[c, g, h][:, i, u, :], ident[:]
+                    )
 
         def gain_x(c, g, h):
-            e_bf[c, g] = e_all[c][:, g * CH : (g + 1) * CH, :]
+            lo = g * CH + h * HALF
             nc.vector.tensor_tensor(
-                out=e_bf[c, g][:, 2 * P * h : 2 * P * (h + 1), :].rearrange("p r (u e) -> p r u e", u=2),
+                out=e_bf[c][:, lo : lo + HALF, :].rearrange("p r (u e) -> p r u e", u=2),
                 in0=xt_bank[c, g, h][:].bitcast(BF16).rearrange("p u (r e) -> p r u e", e=2),
-                in1=gain[:, g, :].rearrange("p (u e) -> p u e", u=2).unsqueeze(1).to_broadcast([P, 2 * P, 2, 2]),
+                in1=gain[:, g, :].rearrange("p (u e) -> p u e", u=2).unsqueeze(1).to_broadcast([P, HALF, 2, 2]),
                 op=ALU.mult,
             )
 
-        def quant_e(c, lo, hi):
+        def quant_e(c, g):
+            cols = slice(g * CH, (g + 1) * CH)
             nc.vector.quantize_mx(
-                out=e_qc[c][:, lo:hi].bitcast(FP8X4),
-                scales=e_sc[c][:, lo:hi],
-                in_=e_all[c][:, lo:hi, :].rearrange("p r t -> p (r t)"),
+                out=e_q[c][:, cols].bitcast(FP8X4),
+                scales=e_s[c][:, cols],
+                in_=e_bf[c][:, cols, :].rearrange("p r t -> p (r t)"),
             )
 
         def enc_pass(c, G, t, g):
             if g == 0:
-                pre_bank[c, G, t] = bank("mm", [P, CH], F32)
+                pre_bank[c, G, t] = bank("mm", [P, CH])
             nc.tensor.matmul_mx(
                 out=pre_bank[c, G, t][:],
                 lhsT=w1[G][:, g, 2 * P * t : 2 * P * (t + 1)].bitcast(FP4X4),
-                lhsT_scale=s1[:, G, g, P * t : P * (t + 1)],
-                rhs=e_q[c, g][:].bitcast(FP8X4),
-                rhs_scale=e_s[c, g][:],
+                lhsT_scale=s1[G][:, g, P * t : P * (t + 1)],
+                rhs=e_q[c][:, g * CH : (g + 1) * CH].bitcast(FP8X4),
+                rhs_scale=e_s[c][:, g * CH : (g + 1) * CH],
                 start=(g == 0),
                 stop=(g == GF - 1),
             )
 
         def relu_slot(c, G, t):
             if t == 0:
-                h_slots[c, G] = work.tile([P, 4, CH], BF16, name="h_slots", bufs=3, align_bytes=64)
+                h_slots[c, G] = work.tile([P, SLOTS, CH], BF16, name="h_slots", bufs=GH, align_bytes=64)
             nc.scalar.activation(
                 out=h_slots[c, G][:, t, :], in_=pre_bank[c, G, t][:], func=ACT.Relu, bias=b1[:, G, t : t + 1]
             )
 
         def encode(c, G):
-            for t in range(4):
+            for t in range(SLOTS):
                 for g in range(GF):
                     enc_pass(c, G, t, g)
                 relu_slot(c, G, t)
 
-        def enc_first(c, G):
-            for t in range(4):
-                enc_pass(c, G, t, 0)
-
-        def enc_second(c, G):
-            for t in range(4):
-                enc_pass(c, G, t, 1)
-                relu_slot(c, G, t)
-
-        def weave_h(c, G, on_scalar=False):
-            dst = il_all[c][:, G * CH : (G + 1) * CH, :].rearrange("p (n i) t -> p n t i", i=4)
-            src = h_slots[c, G][:].rearrange("p t (n i) -> p n t i", i=4)
-            if on_scalar:
-                nc.scalar.copy(out=dst, in_=src)
-            else:
-                nc.vector.tensor_copy(out=dst, in_=src)
-
-        def quant_h(c, G0, G1):
-            nc.vector.quantize_mx(
-                out=h_qc[c][:, G0 * CH : G1 * CH].bitcast(FP8X4),
-                scales=h_sc[c][:, G0 * CH : G1 * CH],
-                in_=il_all[c][:, G0 * CH : G1 * CH, :].rearrange("p n t -> p (n t)"),
+        def weave_h(c, G):
+            nc.vector.tensor_copy(
+                out=h_bf[c][:, G * CH : (G + 1) * CH, :].rearrange("p (n i) t -> p n t i", i=4),
+                in_=h_slots[c, G][:].rearrange("p t (n i) -> p n t i", i=4),
             )
 
-        def logits(c, j):
-            z_bank[c, j] = bank("mm", [P, CH], F32)
+        def quant_h(c, G0, G1):
+            cols = slice(G0 * CH, G1 * CH)
+            nc.vector.quantize_mx(
+                out=h_q[c][:, cols].bitcast(FP8X4),
+                scales=h_s[c][:, cols],
+                in_=h_bf[c][:, cols, :].rearrange("p n t -> p (n t)"),
+            )
+
+        def new_mask():
+            return work.tile([P, CH], F32, name="mask_t", bufs=8, align_bytes=64)
+
+        def column_mask(c, g, j, lo=0, hi=CH):
+            n = TILES * g + j
+            z = bank("mm", [P, hi - lo])
             for G in range(GH):
+                cols = slice(G * CH + lo, G * CH + hi)
                 nc.tensor.matmul_mx(
-                    out=z_bank[c, j][:],
-                    lhsT=w2[:, G, 2 * P * j : 2 * P * (j + 1)].bitcast(FP4X4),
-                    lhsT_scale=s2[:, G, P * j : P * (j + 1)],
-                    rhs=h_q[c, G][:].bitcast(FP8X4),
-                    rhs_scale=h_s[c, G][:],
+                    out=z[:],
+                    lhsT=w2[:, G, 2 * P * n : 2 * P * (n + 1)].bitcast(FP4X4),
+                    lhsT_scale=s2[:, G, P * n : P * (n + 1)],
+                    rhs=h_q[c][:, cols].bitcast(FP8X4),
+                    rhs_scale=h_s[c][:, cols],
                     start=(G == 0),
                     stop=(G == GH - 1),
                 )
-            mask_t[c, j] = work.tile([P, CH], F32, name="mask_t", bufs=8, align_bytes=64)
+            if lo == 0:
+                mask[c, g, j] = new_mask()
+            nc.scalar.activation(out=mask[c, g, j][:, lo:hi], in_=z[:], func=ACT.Sigmoid, bias=b2_cols[:, n : n + 1])
 
-        def sigmoid(c, j, lo=0, hi=CH):
-            nc.scalar.activation(
-                out=mask_t[c, j][:, lo:hi], in_=z_bank[c, j][:, lo:hi], func=ACT.Sigmoid, bias=b2[:, j : j + 1]
-            )
-
-        def masks(c, j0, j1):
+        def column_masks(c, g, j0, j1):
             for j in range(j0, j1):
-                logits(c, j)
-                sigmoid(c, j)
+                column_mask(c, g, j)
 
-        def turn_mask(blk, role="tr"):
-            c, g, h, i0, i1, j0, j1 = blk
-            mask_bank[blk] = bank(role, [P, i1 - i0, (j1 - j0) * P], F32)
+        def row_mask(h, i):
+            z = bank("mm", [P, KP])
+            for G in range(GH):
+                lo = G * CH + h * HALF + i * P
+                nc.tensor.matmul_mx(
+                    out=z[:],
+                    lhsT=h_q[0][:, lo : lo + P].bitcast(FP8X4),
+                    lhsT_scale=h_s[0][:, lo : lo + P],
+                    rhs=w2[:, G, 2 * KP :].bitcast(FP4X4),
+                    rhs_scale=s2[:, G, KP:],
+                    start=(G == 0),
+                    stop=(G == GH - 1),
+                )
+            biased = work.tile([P, KP], F32, name="zf", bufs=3, align_bytes=64)
+            nc.vector.tensor_tensor(out=biased[:], in0=z[:], in1=b2_wide[:], op=ALU.add)
+            mask["row", h, i] = new_mask()
+            nc.scalar.activation(out=mask["row", h, i][:], in_=biased[:], func=ACT.Sigmoid)
+
+        def row_apply(h, i):
+            nc.vector.tensor_tensor(
+                out=y[0, 1, h][:, i, :], in0=mask["row", h, i][:], in1=x[0, 1, h][:, i, :], op=ALU.mult
+            )
+            r0 = h * HALF + i * P
+            nc.sync.dma_start(out=out_0[r0 : r0 + P, KP:], in_=y[0, 1, h][:, i, :])
+
+        def y_view(c, g, h, i0, i1, j0, j1):
+            if c == 0:
+                return y[c, g, h][:, i0:i1, j0 * P : j1 * P]
+            ja = max(a for a, b in Y_PIECES[g] if a <= j0)
+            first = 0 if h is None else 2 * h
+            return y_piece[g, ja][:, first + i0 : first + i1, (j0 - ja) * P : (j1 - ja) * P]
+
+        def frame_tiles(c, g, j0=0, j1=TILES):
+            return [(c, g, h, i, i + 1, j0, j1) for h in range(2) for i in range(2)]
+
+        def half(c, g, h, j0=0, j1=TILES):
+            return (c, g, h, 0, 2, j0, j1)
+
+        def chunk(c, g, j0, j1):
+            return (c, g, None, 0, TILES, j0, j1)
+
+        def turn_mask(patch):
+            c, g, h, i0, i1, j0, j1 = patch
+            mask_bank[patch] = bank("tr", [P, i1 - i0, (j1 - j0) * P])
             for i in range(i0, i1):
-                r0 = (2 * h + i) * P
+                r0 = (0 if h is None else h * HALF) + i * P
                 for j in range(j0, j1):
                     nc.tensor.transpose(
-                        mask_bank[blk][:, i - i0, (j - j0) * P : (j - j0 + 1) * P],
-                        mask_t[c, 4 * g + j][:, r0 : r0 + P],
+                        mask_bank[patch][:, i - i0, (j - j0) * P : (j - j0 + 1) * P],
+                        mask[c, g, j][:, r0 : r0 + P],
                         ident[:],
                     )
 
-        def apply_mask(blk):
-            c, g, h, i0, i1, j0, j1 = blk
+        def apply_mask(patch):
+            c, g, h, i0, i1, j0, j1 = patch
             nc.vector.tensor_tensor(
-                out=y[c, g, h][:, i0:i1, j0 * P : j1 * P],
-                in0=mask_bank[blk][:],
-                in1=x[c, g, h][:, i0:i1, j0 * P : j1 * P],
-                op=ALU.mult,
+                out=y_view(*patch), in0=mask_bank[patch][:], in1=x[c, g, h][:, i0:i1, j0 * P : j1 * P], op=ALU.mult
             )
 
-        def apply_mask_bf(blk):
-            c, g, h, i0, i1, j0, j1 = blk
-            for i in range(i0, i1):
-                nc.vector.tensor_tensor(
-                    out=y_bf[c, g, h][:, i, :, 64 * j0 : 64 * j1].rearrange("p u (m e) -> p u m e", e=2),
-                    in0=mask_bank[blk][:, i - i0, :].rearrange("p (m u e) -> p u m e", u=2, e=2),
-                    in1=x[c, g, h][:, i, j0 * P : j1 * P].rearrange("p (m u e) -> p u m e", u=2, e=2),
-                    op=ALU.mult,
-                )
-
-        def round_y(blk, on_scalar=False):
-            c, g, h, i0, i1, j0, j1 = blk
-            dst = y_bf[c, g, h][:, i0:i1, :, 64 * j0 : 64 * j1].rearrange("p i u (m e) -> p i u m e", e=2)
-            src = y[c, g, h][:, i0:i1, j0 * P : j1 * P].rearrange("p i (m u e) -> p i u m e", u=2, e=2)
-            if on_scalar:
-                nc.scalar.copy(out=dst, in_=src)
-            else:
-                nc.vector.tensor_copy(out=dst, in_=src)
-
-        def store_y(c, g, h, j0=0, j1=4):
+        def store_y(patch):
+            c, g, h, i0, i1, j0, j1 = patch
             rows = out_0[frames(c, h), g * KP + j0 * P : g * KP + j1 * P]
-            nc.sync.dma_start(out=rows.rearrange("(i p) k -> p i k", p=P), in_=y[c, g, h][:, :, j0 * P : j1 * P])
+            nc.sync.dma_start(out=rows.rearrange("(i p) k -> p i k", p=P), in_=y_view(*patch))
 
-        def turn_y(c, g, h, role="mm"):
-            words = y_bf[c, g, h][:].bitcast(F32)
-            yt_bank[c, g, h] = bank(role, [P, 2, 2 * P], F32)
-            for i in range(2):
-                for u in range(2):
-                    nc.tensor.transpose(yt_bank[c, g, h][:, u, i * P : (i + 1) * P], words[:, i, u, :], ident[:])
-
-        def weave_y(c, g, h, on_scalar=True):
-            if h == 0:
-                yt[c, g] = work.tile([P, CH, 2], F32, name="yt", bufs=3, align_bytes=64)
-            dst = yt[c, g][:, 2 * P * h : 2 * P * (h + 1), :]
-            src = yt_bank[c, g, h][:].rearrange("p u r -> p r u")
-            if on_scalar:
-                nc.scalar.copy(out=dst, in_=src)
-            else:
-                nc.vector.tensor_copy(out=dst, in_=src)
-
-        def planes(c, g, lo=0, hi=CH):
-            y_q = work.tile([P, hi - lo], U32, name="y_q", bufs=4, align_bytes=64)
-            nc.vector.quantize_mx(
-                out=y_q[:].bitcast(FP8X4),
-                scales=y_s[:, g, c * CH + lo : c * CH + hi],
-                in_=yt[c, g][:, lo:hi, :].rearrange("p r u -> p (r u)").bitcast(BF16),
-            )
-            dst = out_1[g, :, c * CH + lo : c * CH + hi, :].rearrange("p m t -> p (m t)")
-            nc.sync.dma_start(out=dst.bitcast(I32), in_=y_q[:].bitcast(I32))
-
-        def store_scales(c, spread):
-            fr = frames(c, None)
-            for Q in range(4):
-                dst = out_2[:, 4 * Q : 4 * Q + 4, fr].rearrange("g r n -> r g n")
-                queue = nc.scalar if spread and Q % 2 else nc.sync
-                queue.dma_start(out=dst.bitcast(I32), in_=y_s[32 * Q : 32 * Q + 4, :, fr].bitcast(I32))
-
-        b2_wide = kept("b2_wide", [P, F], BF16)
-        zf_bank, zf, mask_f = {}, {}, {}
-
-        def row_logits(u):
-            c, g, h, i = u
-            r0 = (2 * h + i) * P
-            zf_bank[u] = bank("mm", [P, KP], F32)
-            for G in range(GH):
-                nc.tensor.matmul_mx(
-                    out=zf_bank[u][:],
-                    lhsT=h_q[c, G][:, r0 : r0 + P].bitcast(FP8X4),
-                    lhsT_scale=h_s[c, G][:, r0 : r0 + P],
-                    rhs=w2[:, G, 2 * KP * g : 2 * KP * (g + 1)].bitcast(FP4X4),
-                    rhs_scale=s2[:, G, KP * g : KP * (g + 1)],
-                    start=(G == 0),
-                    stop=(G == GH - 1),
-                )
-
-        def row_bias(u, lo=0, hi=KP):
-            if lo == 0:
-                zf[u] = work.tile([P, KP], F32, name="zf", bufs=3, align_bytes=64)
-            g = u[1]
-            nc.vector.tensor_tensor(
-                out=zf[u][:, lo:hi], in0=zf_bank[u][:, lo:hi], in1=b2_wide[:, g * KP + lo : g * KP + hi], op=ALU.add
+        def round_y(patch, engine):
+            c, g, h, i0, i1, j0, j1 = patch
+            copy_on(
+                engine,
+                y_pairs[c, g, h][:, i0:i1, :, 64 * j0 : 64 * j1].rearrange("p i u (m e) -> p i u m e", e=2),
+                y_view(*patch).rearrange("p i (m u e) -> p i u m e", u=2, e=2),
             )
 
-        def row_sigmoid(u, lo=0, hi=KP):
-            if lo == 0:
-                mask_f[u] = work.tile([P, KP], F32, name="mask_t", bufs=8, align_bytes=64)
-            nc.scalar.activation(out=mask_f[u][:, lo:hi], in_=zf[u][:, lo:hi], func=ACT.Sigmoid)
-
-        def row_apply(u):
-            c, g, h, i = u
-            nc.vector.tensor_tensor(out=y[c, g, h][:, i, :], in0=mask_f[u][:], in1=x[c, g, h][:, i, :], op=ALU.mult)
-            r0 = c * CH + (2 * h + i) * P
-            nc.sync.dma_start(out=out_0[r0 : r0 + P, g * KP : (g + 1) * KP], in_=y[c, g, h][:, i, :])
-
-        def row_apply_bf(u, lo=0, hi=KP):
-            c, g, h, i = u
+        def apply_mask_rounded(patch):
+            c, g, h, i, i1, j0, j1 = patch
             nc.vector.tensor_tensor(
-                out=y_bf[c, g, h][:, i, :, lo // 2 : hi // 2].rearrange("p u (m e) -> p u m e", e=2),
-                in0=mask_f[u][:, lo:hi].rearrange("p (m u e) -> p u m e", u=2, e=2),
-                in1=x[c, g, h][:, i, lo:hi].rearrange("p (m u e) -> p u m e", u=2, e=2),
+                out=y_pairs[c, g, h][:, i, :, 64 * j0 : 64 * j1].rearrange("p u (m e) -> p u m e", e=2),
+                in0=mask_bank[patch][:, 0, :].rearrange("p (m u e) -> p u m e", u=2, e=2),
+                in1=x[c, g, h][:, i, j0 * P : j1 * P].rearrange("p (m u e) -> p u m e", u=2, e=2),
                 op=ALU.mult,
             )
 
-        def row_round(u, on_scalar):
-            c, g, h, i = u
-            round_y((c, g, h, i, i + 1, 0, 4), on_scalar)
-
-        def row_turn(u):
-            c, g, h, i = u
-            words = y_bf[c, g, h][:].bitcast(F32)
-            yt_bank[u] = bank("tr", [P, 2, P], F32)
-            for v in range(2):
-                nc.tensor.transpose(yt_bank[u][:, v, :], words[:, i, v, :], ident[:])
-
-        def row_weave(u, on_scalar=True):
-            c, g, h, i = u
-            if (c, g) not in yt:
-                yt[c, g] = work.tile([P, CH, 2], F32, name="yt", bufs=3, align_bytes=64)
-            r0 = (2 * h + i) * P
-            src = yt_bank[u][:].rearrange("p u r -> p r u")
-            if on_scalar:
-                nc.scalar.copy(out=yt[c, g][:, r0 : r0 + P, :], in_=src)
-            else:
-                nc.vector.tensor_copy(out=yt[c, g][:, r0 : r0 + P, :], in_=src)
-
-        def row_planes(u):
-            c, g, h, i = u
-            r0 = (2 * h + i) * P
-            planes(c, g, r0, r0 + P)
-
-        def turn_col(c, g, j, role="tr"):
-            col = bank(role, [P, 4, P], F32)
-            for n in range(4):
-                nc.tensor.transpose(col[:, n, :], mask_t[c, 4 * g + j][:, n * P : (n + 1) * P], ident[:])
-            mask_bank[c, g, None, 0, 4, j, j + 1] = col
-
-        def row_turn_role(u, role):
-            c, g, h, i = u
-            words = y_bf[c, g, h][:].bitcast(F32)
-            yt_bank[u] = bank(role, [P, 2, P], F32)
-            for v in range(2):
-                nc.tensor.transpose(yt_bank[u][:, v, :], words[:, i, v, :], ident[:])
-
-        def tile_mask(c, j, n):
-            if n == 0:
-                mask_t[c, j] = work.tile([P, CH], F32, name="mask_t", bufs=8, align_bytes=64)
-            z = bank("mm", [P, P], F32)
-            fr = slice(n * P, (n + 1) * P)
-            for G in range(GH):
-                nc.tensor.matmul_mx(
-                    out=z[:],
-                    lhsT=w2[:, G, 2 * P * j : 2 * P * (j + 1)].bitcast(FP4X4),
-                    lhsT_scale=s2[:, G, P * j : P * (j + 1)],
-                    rhs=h_q[c, G][:, fr].bitcast(FP8X4),
-                    rhs_scale=h_s[c, G][:, fr],
-                    start=(G == 0),
-                    stop=(G == GH - 1),
+        def turn_y(c, g, ring):
+            yt[c, g, None] = work.tile([P, CH, 2], F32, name="yt", bufs=3, align_bytes=64)
+            for h in range(2):
+                pairs = y_pairs[c, g, h][:].bitcast(F32)
+                turned = bank(ring, [P, 2, HALF])
+                for i in range(2):
+                    for u in range(2):
+                        nc.tensor.transpose(turned[:, u, i * P : (i + 1) * P], pairs[:, i, u, :], ident[:])
+                nc.scalar.copy(
+                    out=yt[c, g, None][:, HALF * h : HALF * (h + 1), :], in_=turned[:].rearrange("p u r -> p r u")
                 )
-            nc.scalar.activation(out=mask_t[c, j][:, fr], in_=z[:], func=ACT.Sigmoid, bias=b2[:, j : j + 1])
 
-        def bias_columns():
-            b2_bank = bank("mm", [P, P], BF16)
-            nc.tensor.transpose(b2_bank[:], b2_rows[:], ident_bf[:])
-            nc.scalar.copy(out=b2[:], in_=b2_bank[:, 0 : F // P])
+        def turn_y_tile(c, g, h, i):
+            pairs = y_pairs[c, g, h][:].bitcast(F32)
+            yt_bank[h, i] = bank("mm", [P, 2, P])
+            for u in range(2):
+                nc.tensor.transpose(yt_bank[h, i][:, u, :], pairs[:, i, u, :], ident[:])
+
+        def weave_y_tile(c, g, h, i, engine):
+            if i == 0:
+                yt[c, g, h] = work.tile([P, HALF, 2], F32, name="yt_half", align_bytes=64)
+            copy_on(engine, yt[c, g, h][:, i * P : (i + 1) * P, :], yt_bank[h, i][:].rearrange("p u r -> p r u"))
+
+        def planes(c, g, h=None):
+            fr = frames(c, h)
+            codes = work.tile([P, fr.stop - fr.start], U32, name="y_q", bufs=4, align_bytes=64)
+            nc.vector.quantize_mx(
+                out=codes[:].bitcast(FP8X4),
+                scales=y_s[c][:, g, fr.start - c * CH : fr.stop - c * CH],
+                in_=yt[c, g, h][:].rearrange("p r u -> p (r u)").bitcast(BF16),
+            )
+            dst = out_1[g, :, fr, :].rearrange("p m t -> p (m t)")
+            nc.sync.dma_start(out=dst.bitcast(I32), in_=codes[:].bitcast(I32))
+
+        def store_scales(c, queues):
+            for Q in range(4):
+                dst = out_2[:, 4 * Q : 4 * Q + 4, frames(c, None)].rearrange("g r n -> r g n")
+                queues[Q % len(queues)].dma_start(
+                    out=dst.bitcast(I32), in_=y_s[c][32 * Q : 32 * Q + 4, :, :].bitcast(I32)
+                )
 
         nc.vector.memset(s1_raw[:].bitcast(I32), 0)
         nc.vector.memset(warm[:, 0:1], 0.0)
@@ -421,7 +347,7 @@ def tile_masked_spectra_for_mel_h1_kernel(
         nc.gpsimd.memset(b2_rows[:], 0.0)
         make_identity(nc, ident_bf[:])
         nc.gpsimd.memset(s2[:].bitcast(I32), 0)
-        nc.scalar.dma_start(out=gain[:], in_=in_gain.rearrange("(g p t) -> p g t", p=P, t=4))
+        nc.scalar.dma_start(out=gain[:], in_=in_gain.rearrange("(g p t) -> p g t", p=P, t=SLOTS))
         nc.scalar.activation(out=warm[:, 1:2], in_=warm[:, 0:1], func=ACT.Sigmoid)
         load_w1(0)
         load_x(0, 0, 0)
@@ -430,48 +356,47 @@ def tile_masked_spectra_for_mel_h1_kernel(
         load_x(0, 1, 0)
         load_x(0, 1, 1)
         load_w1(1)
-        nc.sync.dma_start(out=b1[:], in_=enc_bias.rearrange("(g p t) -> p g t", p=P, t=4))
+        nc.sync.dma_start(out=b1[:], in_=enc_bias.rearrange("(g p t) -> p g t", p=P, t=SLOTS))
         load_x(1, 0, None)
         load_x(1, 1, None)
         load_w1(2)
         nc.sync.dma_start(out=b2_rows[0 : F // P, :], in_=mask_bias.rearrange("(j p) -> j p", p=P))
         load_scales(s2, mask_scales)
         nc.sync.dma_start(out=w2[:].bitcast(I32), in_=mask_words.rearrange("g p n -> p g n").bitcast(I32))
-        nc.sync.dma_start(out=b2_wide[:, KP:], in_=mask_bias[KP:].partition_broadcast(P))
+        nc.sync.dma_start(out=b2_wide[:], in_=mask_bias[KP:].partition_broadcast(P))
 
+        halves = [(g, h) for g in range(GF) for h in range(2)]
+        for g, h in halves:
+            sort_x(0, g, h)
+            turn_x(0, g, h)
+        sort_w1_codes(0)
         for g in range(GF):
-            for h in range(2):
-                sort_x(0, g, h)
-                turn_x(0, g, h)
-        sort_words(0)
-        gain_x(0, 0, 0)
-        gain_x(0, 0, 1)
-        sort_scales(0, 1)
-        quant_e(0, 0, 512)
-        enc_first(0, 0)
-        gain_x(0, 1, 0)
-        gain_x(0, 1, 1)
-        sort_scales(1, 2)
-        quant_e(0, 512, 1024)
-        for g in range(GF):
-            for h in range(2):
-                sort_x(1, g, h)
-        enc_second(0, 0)
-        sort_words(1)
-        sort_scales(2, 3)
-        for g in range(GF):
-            for h in range(2):
-                turn_x(1, g, h)
-        bias_columns()
+            gain_x(0, g, 0)
+            gain_x(0, g, 1)
+            sort_w1_scales(g)
+            quant_e(0, g)
+            if g == 0:
+                for t in range(SLOTS):
+                    enc_pass(0, 0, t, 0)
+        for g, h in halves:
+            sort_x(1, g, h)
+        for t in range(SLOTS):
+            enc_pass(0, 0, t, 1)
+            relu_slot(0, 0, t)
+        sort_w1_codes(1)
+        sort_w1_scales(2)
+        for g, h in halves:
+            turn_x(1, g, h)
+        b2_bank = bank("mm", [P, P], BF16)
+        nc.tensor.transpose(b2_bank[:], b2_rows[:], ident_bf[:])
+        nc.scalar.copy(out=b2_cols[:], in_=b2_bank[:, 0 : F // P])
         encode(0, 1)
-        sort_words(2)
-        gain_x(1, 0, 0)
-        gain_x(1, 0, 1)
+        sort_w1_codes(2)
         encode(0, 2)
-        gain_x(1, 1, 0)
-        gain_x(1, 1, 1)
-        quant_e(1, 0, 512)
-        quant_e(1, 512, 1024)
+        for g, h in halves:
+            gain_x(1, g, h)
+        for g in range(GF):
+            quant_e(1, g)
         weave_h(0, 0)
         encode(1, 0)
         weave_h(0, 1)
@@ -479,106 +404,86 @@ def tile_masked_spectra_for_mel_h1_kernel(
         weave_h(0, 2)
         encode(1, 1)
         weave_h(1, 0)
-        quant_h(0, 1, 3)
+        quant_h(0, 1, GH)
         encode(1, 2)
 
-        def whole(c, g):
-            return [(c, g, h, i, i + 1, 0, 4) for h in range(2) for i in range(2)]
-        def cols(c, g, j0, j1):
-            return [(c, g, h, 0, 2, j0, j1) for h in range(2)]
-        def finish(c, g):
-            for h in range(2):
-                apply_mask((c, g, h, 0, 1, 0, 4))
-                apply_mask((c, g, h, 1, 2, 0, 4))
-                store_y(c, g, h)
-            for h in range(2):
-                round_y((c, g, h, 0, 2, 0, 4))
-        def close(c, g, role="mm"):
-            for h in range(2):
-                turn_y(c, g, h, role)
-                weave_y(c, g, h)
-
-        def col(c, g, j):
-            return (c, g, None, 0, 4, j, j + 1)
-        def half(c, g, h, j0=0, j1=4):
-            return (c, g, h, 0, 2, j0, j1)
-        rows = [(0, 1, h, i) for h in range(2) for i in range(2)]
-        def row_mask(u):
-            row_logits(u)
-            row_bias(u)
-            row_sigmoid(u)
-        masks(0, 0, 4)
+        column_masks(0, 0, 0, TILES)
         weave_h(1, 1)
         quant_h(1, 0, 1)
         weave_h(1, 2)
-        quant_h(1, 1, 3)
-        for u in rows[:2]:
-            row_mask(u)
-        first = whole(0, 0)
-        for b in first:
-            turn_mask(b)
+        quant_h(1, 1, GH)
+        row_mask(0, 0)
+        row_mask(0, 1)
+        first = frame_tiles(0, 0)
+        for patch in first:
+            turn_mask(patch)
         apply_mask(first[0])
         apply_mask(first[1])
-        store_y(0, 0, 0)
-        round_y(half(0, 0, 0), True)
+        store_y(half(0, 0, 0))
+        round_y(half(0, 0, 0), "scalar")
         apply_mask(first[2])
-        row_mask(rows[2])
+        row_mask(1, 0)
         apply_mask(first[3])
-        store_y(0, 0, 1)
-        row_mask(rows[3])
-        round_y(half(0, 0, 1))
-        masks(1, 0, 4)
-        for u in rows:
-            row_apply(u)
-        close(0, 0)
-        for b in cols(1, 0, 0, 2):
-            turn_mask(b)
-        turn_col(1, 0, 2)
-        round_y(half(0, 1, 1), True)
-        round_y(half(0, 1, 0))
-        for b in cols(1, 0, 0, 2):
-            apply_mask(b)
-        planes(0, 0)
-        apply_mask(col(1, 0, 2))
-        store_y(1, 0, None, 0, 3)
-        masks(1, 4, 6)
-        turn_col(1, 0, 3)
-        close(0, 1)
-        turn_col(1, 1, 0)
-        apply_mask(col(1, 0, 3))
-        store_y(1, 0, None, 3, 4)
-        round_y(half(1, 0, 0))
-        round_y(half(1, 0, 1))
-        apply_mask(col(1, 1, 0))
-        masks(1, 6, 7)
-        turn_col(1, 1, 1)
-        close(1, 0, "tr")
-        turn_col(1, 1, 2)
-        planes(0, 1)
-        store_scales(0, False)
-        apply_mask(col(1, 1, 1))
-        store_y(1, 1, None, 0, 2)
+        store_y(half(0, 0, 1))
+        row_mask(1, 1)
+        round_y(half(0, 0, 1), "vector")
+        column_masks(1, 0, 0, TILES)
+        for h in range(2):
+            for i in range(2):
+                row_apply(h, i)
 
-        for n in range(4):
-            tile_mask(1, 7, n)
-        apply_mask(col(1, 1, 2))
-        store_y(1, 1, None, 2, 3)
+        turn_y(0, 0, "mm")
+        for h in range(2):
+            turn_mask(half(1, 0, h, 0, 2))
+        turn_mask(chunk(1, 0, 2, 3))
+        round_y(half(0, 1, 1), "scalar")
+        round_y(half(0, 1, 0), "vector")
+        for h in range(2):
+            apply_mask(half(1, 0, h, 0, 2))
+            store_y(half(1, 0, h, 0, 2))
+        planes(0, 0)
+        apply_mask(chunk(1, 0, 2, 3))
+        round_y(chunk(1, 0, 0, 2), "vector")
+
+        column_masks(1, 1, 0, 2)
+        turn_mask(chunk(1, 0, 3, 4))
+        turn_y(0, 1, "mm")
+        turn_mask(chunk(1, 1, 0, 1))
+        apply_mask(chunk(1, 0, 3, 4))
+        store_y(chunk(1, 0, 2, 4))
+        round_y(chunk(1, 0, 2, 4), "vector")
+        apply_mask(chunk(1, 1, 0, 1))
+
+        column_mask(1, 1, 2)
+        turn_mask(chunk(1, 1, 1, 2))
+        turn_y(1, 0, "tr")
+        turn_mask(chunk(1, 1, 2, 3))
+        planes(0, 1)
+        store_scales(0, [nc.sync])
+        apply_mask(chunk(1, 1, 1, 2))
+        store_y(chunk(1, 1, 0, 2))
+        for h in range(2):
+            round_y(half(1, 1, h, 0, 2), "vector")
+
+        for lo in range(0, CH, P):
+            column_mask(1, 1, 3, lo, lo + P)
+        apply_mask(chunk(1, 1, 2, 3))
+        store_y(chunk(1, 1, 2, 3))
         planes(1, 0)
-        round_y(half(1, 1, 0, 0, 3))
-        round_y(half(1, 1, 1, 0, 3), True)
-        last = [(1, 1, h, i) for h in range(2) for i in range(2)]
-        blocks = [(1, 1, h, i, i + 1, 3, 4) for h in range(2) for i in range(2)]
-        for b in blocks:
-            turn_mask(b, "tr")
-        for b in blocks:
-            apply_mask_bf(b)
-        for u in last:
-            row_turn_role(u, "mm")
-        for b in blocks:
-            apply_mask(b)
-        store_y(1, 1, None, 3, 4)
-        for n, u in enumerate(last):
-            row_weave(u, n != 2)
-        planes(1, 1, 0, 256)
-        planes(1, 1, 256, 512)
-        store_scales(1, True)
+        round_y(half(1, 1, 0, 2, 3), "scalar")
+        round_y(half(1, 1, 1, 2, 3), "scalar")
+        last = frame_tiles(1, 1, 3, 4)
+        for patch in last:
+            turn_mask(patch)
+        for patch in last:
+            apply_mask_rounded(patch)
+        for patch in last:
+            turn_y_tile(*patch[:4])
+        for patch in last:
+            apply_mask(patch)
+        store_y(chunk(1, 1, 3, 4))
+        for patch, engine in zip(last, ("scalar", "scalar", "vector", "scalar")):
+            weave_y_tile(*patch[:4], engine)
+        for h in range(2):
+            planes(1, 1, h)
+        store_scales(1, [nc.sync, nc.scalar])

from contextlib import ExitStack

import concourse.mybir as mybir
from concourse.masks import make_identity

T, F, H = 1024, 1024, 1536
FLOPS = 2 * T * F * H * 2

F32 = mybir.dt.float32
BF16 = mybir.dt.bfloat16
I32 = mybir.dt.int32
U32 = mybir.dt.uint32
U8 = mybir.dt.uint8
FP8X4 = mybir.dt.float8_e4m3fn_x4
FP4X4 = mybir.dt.float4_e2m1fn_x4
ACT = mybir.ActivationFunctionType
ALU = mybir.AluOpType

P = 128
SLOTS = 4
KP = P * SLOTS
CH = 512
HALF = CH // 2
TILES = CH // P
NCH, GF, GH = T // CH, F // KP, H // KP
RING = 4
Y_PIECES = ([(0, 2), (2, 4)], [(0, 2), (2, 3), (3, 4)])


def tile_masked_spectra_for_mel_h1_kernel(
    tc, spec, in_gain, enc_words, enc_scales, enc_bias, mask_words, mask_scales, mask_bias, out_0, out_1, out_2
):
    nc = tc.nc
    with ExitStack() as ctx:
        keep = ctx.enter_context(tc.tile_pool(name="keep", bufs=1))
        work = ctx.enter_context(tc.tile_pool(name="work", bufs=2))
        psum = ctx.enter_context(tc.psum_pool(name="psum", bufs=1))
        ctx.enter_context(tc.manual_schedule())

        taken = {"mm": 0, "tr": 0}

        def bank(ring, shape, dtype=F32):
            k = taken[ring] % RING
            taken[ring] = taken[ring] + 1
            return psum.tile(shape, dtype, name="%s%d" % (ring, k))

        def kept(name, shape, dtype):
            return keep.tile(shape, dtype, name=name, align_bytes=64)

        def copy_on(engine, out, in_):
            if engine == "scalar":
                nc.scalar.copy(out=out, in_=in_)
            else:
                nc.vector.tensor_copy(out=out, in_=in_)

        x, y, y_piece, y_pairs = {}, {}, {}, {}
        for g in range(GF):
            for h in range(2):
                x[0, g, h] = kept("x0%d%d" % (g, h), [P, 2, KP], BF16)
                y[0, g, h] = kept("y0%d%d" % (g, h), [P, 2, KP], F32)
                y_pairs[0, g, h] = kept("y_pairs0%d%d" % (g, h), [P, 2, 2, HALF], BF16)
            x[1, g, None] = kept("x1%d" % g, [P, TILES, KP], BF16)
            for h in range(2):
                x[1, g, h] = x[1, g, None][:, 2 * h : 2 * h + 2, :]
            for ja, jb in Y_PIECES[g]:
                y_piece[g, ja] = kept("y1%d%d" % (g, ja), [P, TILES, (jb - ja) * P], F32)
        y_pairs[1, 0, None] = kept("y_pairs10", [P, TILES, 2, HALF], BF16)
        for h in range(2):
            y_pairs[1, 0, h] = y_pairs[1, 0, None][:, 2 * h : 2 * h + 2, :, :]
            y_pairs[1, 1, h] = kept("y_pairs11%d" % h, [P, 2, 2, HALF], BF16)

        gain = kept("gain", [P, GF, SLOTS], BF16)
        b1 = kept("b1", [P, GH, SLOTS], BF16)
        b2_rows = kept("b2_rows", [P, P], BF16)
        b2_cols = kept("b2_cols", [P, F // P], F32)
        b2_wide = kept("b2_wide", [P, KP], BF16)
        ident = kept("ident", [P, P], F32)
        ident_bf = kept("ident_bf", [P, P], BF16)
        warm = kept("warm", [P, 2], F32)
        w1_raw = [kept("w1_raw%d" % G, [P, GF, 2 * KP], U8) for G in range(GH)]
        s1_raw = kept("s1_raw", [P, GF, H], U8)
        w1 = [kept("w1_%d" % G, [P, GF, 2 * KP], U8) for G in range(GH)]
        s1 = [kept("s1_%d" % G, [P, GF, KP], U8) for G in range(GH)]
        w2 = kept("w2", [P, GH, 2 * F], U8)
        s2 = kept("s2", [P, GH, F], U8)
        e_bf = [kept("e_bf%d" % c, [P, GF * CH, SLOTS], BF16) for c in range(NCH)]
        e_q = [kept("e_q%d" % c, [P, GF * CH], U32) for c in range(NCH)]
        e_s = [kept("e_s%d" % c, [P, GF * CH], U8) for c in range(NCH)]
        h_bf = [kept("h_il%d" % c, [P, GH * CH, SLOTS], BF16) for c in range(NCH)]
        h_q = [kept("h_q%d" % c, [P, GH * CH], U32) for c in range(NCH)]
        h_s = [kept("h_s%d" % c, [P, GH * CH], U8) for c in range(NCH)]
        y_s = [kept("y_s%d" % c, [P, GF, CH], U8) for c in range(NCH)]
        x_pairs, xt_bank, pre_bank, h_slots = {}, {}, {}, {}
        mask, mask_bank, yt_bank, yt = {}, {}, {}, {}

        def frames(c, h):
            if h is None:
                return slice(c * CH, (c + 1) * CH)
            return slice(c * CH + HALF * h, c * CH + HALF * (h + 1))

        def load_x(c, g, h):
            rows = spec[frames(c, h), g * KP : (g + 1) * KP]
            nc.sync.dma_start(out=x[c, g, h][:], in_=rows.rearrange("(i p) k -> p i k", p=P))

        def load_w1(G):
            src = enc_words[:, :, 2 * KP * G : 2 * KP * (G + 1)].rearrange("g p n -> p g n")
            nc.sync.dma_start(out=w1_raw[G][:].bitcast(I32), in_=src.bitcast(I32))

        def load_scales(tile, scales):
            for Q in range(4):
                src = scales[:, 4 * Q : 4 * Q + 4, :].rearrange("g r n -> r g n")
                nc.sync.dma_start(out=tile[32 * Q : 32 * Q + 4, :, :].bitcast(I32), in_=src.bitcast(I32))

        def sort_w1_codes(G):
            nc.vector.tensor_copy(
                out=w1[G][:].rearrange("p g (t m b) -> p g t m b", t=SLOTS, b=2),
                in_=w1_raw[G][:].rearrange("p g (m t b) -> p g t m b", t=SLOTS, b=2),
            )

        def sort_w1_scales(G):
            nc.vector.tensor_copy(
                out=s1[G][:].rearrange("p g (t m) -> p g t m", t=SLOTS),
                in_=s1_raw[:, :, KP * G : KP * (G + 1)].rearrange("p g (m t) -> p g t m", t=SLOTS),
            )

        def sort_x(c, g, h):
            x_pairs[c, g, h] = work.tile([P, 2, 2, P], F32, name="x_sorted", bufs=4, align_bytes=64)
            nc.scalar.copy(
                out=x_pairs[c, g, h][:], in_=x[c, g, h][:].bitcast(F32).rearrange("p i (m u) -> p i u m", u=2)
            )

        def turn_x(c, g, h):
            xt_bank[c, g, h] = bank("tr", [P, 2, HALF])
            for i in range(2):
                for u in range(2):
                    nc.tensor.transpose(
                        xt_bank[c, g, h][:, u, i * P : (i + 1) * P], x_pairs[c, g, h][:, i, u, :], ident[:]
                    )

        def gain_x(c, g, h):
            lo = g * CH + h * HALF
            nc.vector.tensor_tensor(
                out=e_bf[c][:, lo : lo + HALF, :].rearrange("p r (u e) -> p r u e", u=2),
                in0=xt_bank[c, g, h][:].bitcast(BF16).rearrange("p u (r e) -> p r u e", e=2),
                in1=gain[:, g, :].rearrange("p (u e) -> p u e", u=2).unsqueeze(1).to_broadcast([P, HALF, 2, 2]),
                op=ALU.mult,
            )

        def quant_e(c, g):
            cols = slice(g * CH, (g + 1) * CH)
            nc.vector.quantize_mx(
                out=e_q[c][:, cols].bitcast(FP8X4),
                scales=e_s[c][:, cols],
                in_=e_bf[c][:, cols, :].rearrange("p r t -> p (r t)"),
            )

        def enc_pass(c, G, t, g):
            if g == 0:
                pre_bank[c, G, t] = bank("mm", [P, CH])
            nc.tensor.matmul_mx(
                out=pre_bank[c, G, t][:],
                lhsT=w1[G][:, g, 2 * P * t : 2 * P * (t + 1)].bitcast(FP4X4),
                lhsT_scale=s1[G][:, g, P * t : P * (t + 1)],
                rhs=e_q[c][:, g * CH : (g + 1) * CH].bitcast(FP8X4),
                rhs_scale=e_s[c][:, g * CH : (g + 1) * CH],
                start=(g == 0),
                stop=(g == GF - 1),
            )

        def relu_slot(c, G, t):
            if t == 0:
                h_slots[c, G] = work.tile([P, SLOTS, CH], BF16, name="h_slots", bufs=GH, align_bytes=64)
            nc.scalar.activation(
                out=h_slots[c, G][:, t, :], in_=pre_bank[c, G, t][:], func=ACT.Relu, bias=b1[:, G, t : t + 1]
            )

        def encode(c, G):
            for t in range(SLOTS):
                for g in range(GF):
                    enc_pass(c, G, t, g)
                relu_slot(c, G, t)

        def weave_h(c, G):
            nc.vector.tensor_copy(
                out=h_bf[c][:, G * CH : (G + 1) * CH, :].rearrange("p (n i) t -> p n t i", i=4),
                in_=h_slots[c, G][:].rearrange("p t (n i) -> p n t i", i=4),
            )

        def quant_h(c, G0, G1):
            cols = slice(G0 * CH, G1 * CH)
            nc.vector.quantize_mx(
                out=h_q[c][:, cols].bitcast(FP8X4),
                scales=h_s[c][:, cols],
                in_=h_bf[c][:, cols, :].rearrange("p n t -> p (n t)"),
            )

        def new_mask():
            return work.tile([P, CH], F32, name="mask_t", bufs=8, align_bytes=64)

        def column_mask(c, g, j, lo=0, hi=CH):
            n = TILES * g + j
            z = bank("mm", [P, hi - lo])
            for G in range(GH):
                cols = slice(G * CH + lo, G * CH + hi)
                nc.tensor.matmul_mx(
                    out=z[:],
                    lhsT=w2[:, G, 2 * P * n : 2 * P * (n + 1)].bitcast(FP4X4),
                    lhsT_scale=s2[:, G, P * n : P * (n + 1)],
                    rhs=h_q[c][:, cols].bitcast(FP8X4),
                    rhs_scale=h_s[c][:, cols],
                    start=(G == 0),
                    stop=(G == GH - 1),
                )
            if lo == 0:
                mask[c, g, j] = new_mask()
            nc.scalar.activation(out=mask[c, g, j][:, lo:hi], in_=z[:], func=ACT.Sigmoid, bias=b2_cols[:, n : n + 1])

        def column_masks(c, g, j0, j1):
            for j in range(j0, j1):
                column_mask(c, g, j)

        def row_mask(h, i):
            z = bank("mm", [P, KP])
            for G in range(GH):
                lo = G * CH + h * HALF + i * P
                nc.tensor.matmul_mx(
                    out=z[:],
                    lhsT=h_q[0][:, lo : lo + P].bitcast(FP8X4),
                    lhsT_scale=h_s[0][:, lo : lo + P],
                    rhs=w2[:, G, 2 * KP :].bitcast(FP4X4),
                    rhs_scale=s2[:, G, KP:],
                    start=(G == 0),
                    stop=(G == GH - 1),
                )
            biased = work.tile([P, KP], F32, name="zf", bufs=3, align_bytes=64)
            nc.vector.tensor_tensor(out=biased[:], in0=z[:], in1=b2_wide[:], op=ALU.add)
            mask["row", h, i] = new_mask()
            nc.scalar.activation(out=mask["row", h, i][:], in_=biased[:], func=ACT.Sigmoid)

        def row_apply(h, i):
            nc.vector.tensor_tensor(
                out=y[0, 1, h][:, i, :], in0=mask["row", h, i][:], in1=x[0, 1, h][:, i, :], op=ALU.mult
            )
            r0 = h * HALF + i * P
            nc.sync.dma_start(out=out_0[r0 : r0 + P, KP:], in_=y[0, 1, h][:, i, :])

        def y_view(c, g, h, i0, i1, j0, j1):
            if c == 0:
                return y[c, g, h][:, i0:i1, j0 * P : j1 * P]
            ja = max(a for a, b in Y_PIECES[g] if a <= j0)
            first = 0 if h is None else 2 * h
            return y_piece[g, ja][:, first + i0 : first + i1, (j0 - ja) * P : (j1 - ja) * P]

        def frame_tiles(c, g, j0=0, j1=TILES):
            return [(c, g, h, i, i + 1, j0, j1) for h in range(2) for i in range(2)]

        def half(c, g, h, j0=0, j1=TILES):
            return (c, g, h, 0, 2, j0, j1)

        def chunk(c, g, j0, j1):
            return (c, g, None, 0, TILES, j0, j1)

        def turn_mask(patch):
            c, g, h, i0, i1, j0, j1 = patch
            mask_bank[patch] = bank("tr", [P, i1 - i0, (j1 - j0) * P])
            for i in range(i0, i1):
                r0 = (0 if h is None else h * HALF) + i * P
                for j in range(j0, j1):
                    nc.tensor.transpose(
                        mask_bank[patch][:, i - i0, (j - j0) * P : (j - j0 + 1) * P],
                        mask[c, g, j][:, r0 : r0 + P],
                        ident[:],
                    )

        def apply_mask(patch):
            c, g, h, i0, i1, j0, j1 = patch
            nc.vector.tensor_tensor(
                out=y_view(*patch), in0=mask_bank[patch][:], in1=x[c, g, h][:, i0:i1, j0 * P : j1 * P], op=ALU.mult
            )

        def store_y(patch):
            c, g, h, i0, i1, j0, j1 = patch
            rows = out_0[frames(c, h), g * KP + j0 * P : g * KP + j1 * P]
            nc.sync.dma_start(out=rows.rearrange("(i p) k -> p i k", p=P), in_=y_view(*patch))

        def round_y(patch, engine):
            c, g, h, i0, i1, j0, j1 = patch
            copy_on(
                engine,
                y_pairs[c, g, h][:, i0:i1, :, 64 * j0 : 64 * j1].rearrange("p i u (m e) -> p i u m e", e=2),
                y_view(*patch).rearrange("p i (m u e) -> p i u m e", u=2, e=2),
            )

        def apply_mask_rounded(patch):
            c, g, h, i, i1, j0, j1 = patch
            nc.vector.tensor_tensor(
                out=y_pairs[c, g, h][:, i, :, 64 * j0 : 64 * j1].rearrange("p u (m e) -> p u m e", e=2),
                in0=mask_bank[patch][:, 0, :].rearrange("p (m u e) -> p u m e", u=2, e=2),
                in1=x[c, g, h][:, i, j0 * P : j1 * P].rearrange("p (m u e) -> p u m e", u=2, e=2),
                op=ALU.mult,
            )

        def turn_y(c, g, ring):
            yt[c, g, None] = work.tile([P, CH, 2], F32, name="yt", bufs=3, align_bytes=64)
            for h in range(2):
                pairs = y_pairs[c, g, h][:].bitcast(F32)
                turned = bank(ring, [P, 2, HALF])
                for i in range(2):
                    for u in range(2):
                        nc.tensor.transpose(turned[:, u, i * P : (i + 1) * P], pairs[:, i, u, :], ident[:])
                nc.scalar.copy(
                    out=yt[c, g, None][:, HALF * h : HALF * (h + 1), :], in_=turned[:].rearrange("p u r -> p r u")
                )

        def turn_y_tile(c, g, h, i):
            pairs = y_pairs[c, g, h][:].bitcast(F32)
            yt_bank[h, i] = bank("mm", [P, 2, P])
            for u in range(2):
                nc.tensor.transpose(yt_bank[h, i][:, u, :], pairs[:, i, u, :], ident[:])

        def weave_y_tile(c, g, h, i, engine):
            if i == 0:
                yt[c, g, h] = work.tile([P, HALF, 2], F32, name="yt_half", align_bytes=64)
            copy_on(engine, yt[c, g, h][:, i * P : (i + 1) * P, :], yt_bank[h, i][:].rearrange("p u r -> p r u"))

        def planes(c, g, h=None):
            fr = frames(c, h)
            codes = work.tile([P, fr.stop - fr.start], U32, name="y_q", bufs=4, align_bytes=64)
            nc.vector.quantize_mx(
                out=codes[:].bitcast(FP8X4),
                scales=y_s[c][:, g, fr.start - c * CH : fr.stop - c * CH],
                in_=yt[c, g, h][:].rearrange("p r u -> p (r u)").bitcast(BF16),
            )
            dst = out_1[g, :, fr, :].rearrange("p m t -> p (m t)")
            nc.sync.dma_start(out=dst.bitcast(I32), in_=codes[:].bitcast(I32))

        def store_scales(c, queues):
            for Q in range(4):
                dst = out_2[:, 4 * Q : 4 * Q + 4, frames(c, None)].rearrange("g r n -> r g n")
                queues[Q % len(queues)].dma_start(
                    out=dst.bitcast(I32), in_=y_s[c][32 * Q : 32 * Q + 4, :, :].bitcast(I32)
                )

        nc.vector.memset(s1_raw[:].bitcast(I32), 0)
        nc.vector.memset(warm[:, 0:1], 0.0)
        make_identity(nc, ident[:])
        nc.gpsimd.memset(b2_rows[:], 0.0)
        make_identity(nc, ident_bf[:])
        nc.gpsimd.memset(s2[:].bitcast(I32), 0)
        nc.scalar.dma_start(out=gain[:], in_=in_gain.rearrange("(g p t) -> p g t", p=P, t=SLOTS))
        nc.scalar.activation(out=warm[:, 1:2], in_=warm[:, 0:1], func=ACT.Sigmoid)
        load_w1(0)
        load_x(0, 0, 0)
        load_x(0, 0, 1)
        load_scales(s1_raw, enc_scales)
        load_x(0, 1, 0)
        load_x(0, 1, 1)
        load_w1(1)
        nc.sync.dma_start(out=b1[:], in_=enc_bias.rearrange("(g p t) -> p g t", p=P, t=SLOTS))
        load_x(1, 0, None)
        load_x(1, 1, None)
        load_w1(2)
        nc.sync.dma_start(out=b2_rows[0 : F // P, :], in_=mask_bias.rearrange("(j p) -> j p", p=P))
        load_scales(s2, mask_scales)
        nc.sync.dma_start(out=w2[:].bitcast(I32), in_=mask_words.rearrange("g p n -> p g n").bitcast(I32))
        nc.sync.dma_start(out=b2_wide[:], in_=mask_bias[KP:].partition_broadcast(P))

        halves = [(g, h) for g in range(GF) for h in range(2)]
        for g, h in halves:
            sort_x(0, g, h)
            turn_x(0, g, h)
        sort_w1_codes(0)
        for g in range(GF):
            gain_x(0, g, 0)
            gain_x(0, g, 1)
            sort_w1_scales(g)
            quant_e(0, g)
            if g == 0:
                for t in range(SLOTS):
                    enc_pass(0, 0, t, 0)
        for g, h in halves:
            sort_x(1, g, h)
        for t in range(SLOTS):
            enc_pass(0, 0, t, 1)
            relu_slot(0, 0, t)
        sort_w1_codes(1)
        sort_w1_scales(2)
        for g, h in halves:
            turn_x(1, g, h)
        b2_bank = bank("mm", [P, P], BF16)
        nc.tensor.transpose(b2_bank[:], b2_rows[:], ident_bf[:])
        nc.scalar.copy(out=b2_cols[:], in_=b2_bank[:, 0 : F // P])
        encode(0, 1)
        sort_w1_codes(2)
        encode(0, 2)
        for g, h in halves:
            gain_x(1, g, h)
        for g in range(GF):
            quant_e(1, g)
        weave_h(0, 0)
        encode(1, 0)
        weave_h(0, 1)
        quant_h(0, 0, 1)
        weave_h(0, 2)
        encode(1, 1)
        weave_h(1, 0)
        quant_h(0, 1, GH)
        encode(1, 2)

        column_masks(0, 0, 0, TILES)
        weave_h(1, 1)
        quant_h(1, 0, 1)
        weave_h(1, 2)
        quant_h(1, 1, GH)
        row_mask(0, 0)
        row_mask(0, 1)
        first = frame_tiles(0, 0)
        for patch in first:
            turn_mask(patch)
        apply_mask(first[0])
        apply_mask(first[1])
        store_y(half(0, 0, 0))
        round_y(half(0, 0, 0), "scalar")
        apply_mask(first[2])
        row_mask(1, 0)
        apply_mask(first[3])
        store_y(half(0, 0, 1))
        row_mask(1, 1)
        round_y(half(0, 0, 1), "vector")
        column_masks(1, 0, 0, TILES)
        for h in range(2):
            for i in range(2):
                row_apply(h, i)

        turn_y(0, 0, "mm")
        for h in range(2):
            turn_mask(half(1, 0, h, 0, 2))
        turn_mask(chunk(1, 0, 2, 3))
        round_y(half(0, 1, 1), "scalar")
        round_y(half(0, 1, 0), "vector")
        for h in range(2):
            apply_mask(half(1, 0, h, 0, 2))
            store_y(half(1, 0, h, 0, 2))
        planes(0, 0)
        apply_mask(chunk(1, 0, 2, 3))
        round_y(chunk(1, 0, 0, 2), "vector")

        column_masks(1, 1, 0, 2)
        turn_mask(chunk(1, 0, 3, 4))
        turn_y(0, 1, "mm")
        turn_mask(chunk(1, 1, 0, 1))
        apply_mask(chunk(1, 0, 3, 4))
        store_y(chunk(1, 0, 2, 4))
        round_y(chunk(1, 0, 2, 4), "vector")
        apply_mask(chunk(1, 1, 0, 1))

        column_mask(1, 1, 2)
        turn_mask(chunk(1, 1, 1, 2))
        turn_y(1, 0, "tr")
        turn_mask(chunk(1, 1, 2, 3))
        planes(0, 1)
        store_scales(0, [nc.sync])
        apply_mask(chunk(1, 1, 1, 2))
        store_y(chunk(1, 1, 0, 2))
        for h in range(2):
            round_y(half(1, 1, h, 0, 2), "vector")

        for lo in range(0, CH, P):
            column_mask(1, 1, 3, lo, lo + P)
        apply_mask(chunk(1, 1, 2, 3))
        store_y(chunk(1, 1, 2, 3))
        planes(1, 0)
        round_y(half(1, 1, 0, 2, 3), "scalar")
        round_y(half(1, 1, 1, 2, 3), "scalar")
        last = frame_tiles(1, 1, 3, 4)
        for patch in last:
            turn_mask(patch)
        for patch in last:
            apply_mask_rounded(patch)
        for patch in last:
            turn_y_tile(*patch[:4])
        for patch in last:
            apply_mask(patch)
        store_y(chunk(1, 1, 3, 4))
        for patch, engine in zip(last, ("scalar", "scalar", "vector", "scalar")):
            weave_y_tile(*patch[:4], engine)
        for h in range(2):
            planes(1, 1, h)
        store_scales(1, [nc.sync, nc.scalar])
